import numpy as np
import ml_dtypes


def mxq(x, axis, fmt="e4m3"):
    dtype, down = {"e4m3": (ml_dtypes.float8_e4m3fn, 7), "e5m2": (ml_dtypes.float8_e5m2, 14)}[fmt]
    v = np.moveaxis(np.asarray(x, np.float32).astype(ml_dtypes.bfloat16).astype(np.float64), axis, -1)
    blocks = v.reshape(v.shape[:-1] + (-1, 32))
    amax = np.abs(blocks).max(-1, keepdims=True)
    byte = np.maximum(np.where(amax > 0, np.frexp(amax)[1] - 1 + 127, 0) - down, 1)
    scale = np.exp2(byte - 127.0)
    codes = (blocks / scale).astype(np.float32).astype(dtype).astype(np.float64)
    return np.moveaxis((codes * scale).reshape(v.shape), -1, axis)


WIDE = False


def mx_kscale(k):
    if not WIDE:
        return np.ones(k)
    levels = np.array([24, -24, 12, -12, 0])
    if k % 512:
        return np.exp2(np.random.permutation(np.resize(levels, k // 32))).repeat(32)
    a = np.empty((k // 512, 16))
    for p in range(k // 512):
        a[p, :8] = np.random.permutation(np.resize(levels, 8))
        for g in range(8):
            far = levels[np.abs(levels - a[p, g]) >= 10]
            a[p, g + 8] = far[np.random.randint(len(far))]
    return np.exp2(a.ravel()).repeat(32)


def f64(x):
    return np.asarray(x).astype(np.float64)


def striped(idx):
    return np.tile(idx.reshape(-1, 16).T, (8, 1)).astype(np.uint16)


def unstriped(offs):
    return offs[:16].T.reshape(-1).astype(np.int64)


E2M1 = np.array([0.0, 0.5, 1.0, 1.5, 2.0, 3.0, 4.0, 6.0, -0.0, -0.5, -1.0, -1.5, -2.0, -3.0, -4.0, -6.0])


def pack_weight(w, fmt):
    k, n = w.shape
    w = f64(np.asarray(w, np.float32).astype(ml_dtypes.bfloat16)).reshape(k // 32, 32, n)
    amax = np.abs(w).max(1)
    if fmt == "e4m3":
        byte = np.frexp(amax)[1] - 1 + 127 - 7
    else:
        mant, ex = np.frexp(amax / 6.0)
        byte = np.where(mant > 0.5, ex, ex - 1) + 127
    byte = np.clip(np.where(amax > 0, byte, 1), 1, 254)
    scaled = (w * np.exp2(127.0 - byte)[:, None, :]).reshape(k, n).astype(np.float32)
    by_word = np.ascontiguousarray(scaled.reshape(k // 512, 128, 4, n).transpose(0, 1, 3, 2))
    if fmt == "e4m3":
        words = by_word.astype(ml_dtypes.float8_e4m3fn).view(np.uint8)
    else:
        c = by_word.astype(ml_dtypes.float4_e2m1fn).view(np.uint8) & 0xF
        words = (c[..., 0::2] | (c[..., 1::2] << 4)).reshape(k // 512, 128, 2 * n)
    return np.ascontiguousarray(words), np.ascontiguousarray(byte.astype(np.uint8).reshape(k // 512, 16, n))


def unpack_weight(words, scales, fmt):
    g, _, n = scales.shape
    words = np.ascontiguousarray(words).reshape(g, 128, n, -1)
    if fmt == "e4m3":
        vals = words.view(ml_dtypes.float8_e4m3fn).astype(np.float64)
    else:
        nib = np.empty((g, 128, n, 4), np.uint8)
        nib[..., 0::2] = words & 0xF
        nib[..., 1::2] = words >> 4
        vals = E2M1[nib]
    vals = vals * np.repeat(np.exp2(scales.astype(np.float64) - 127.0), 8, axis=1)[..., None]
    return vals.transpose(0, 1, 3, 2).reshape(g * 512, n)


K, R, N, T, J = 1024, 512, 512, 2048, 1024


def setup_inputs():
    n = np.random.standard_normal
    s = mx_kscale(K)[:, None]
    u = mx_kscale(R)[:, None]
    p_tab = pack_weight(n((K, T)) * s, "e4m3")
    p_ws = pack_weight(n((K, R)) / np.sqrt(2 * K) / s * u.T, "e2m1")
    p_wt = pack_weight(n((K, R)) / np.sqrt(2 * K) / s * u.T, "e4m3")
    p_wd = pack_weight(n((R, N)) / np.sqrt(R) / u, "e4m3")
    return {
        "tab_words": p_tab[0],
        "tab_scales": p_tab[1],
        "ws_words": p_ws[0],
        "ws_scales": p_ws[1],
        "wt_words": p_wt[0],
        "wt_scales": p_wt[1],
        "wd_words": p_wd[0],
        "wd_scales": p_wd[1],
        "b": (0.3 * n(N)).astype(np.float32),
        "wgo": np.tile(np.random.uniform(0.5, 2.0, J), (128, 1)).astype(np.float32),
        "offs": striped(np.random.permutation(T)[:J]),
        "offs2": striped(np.random.permutation(T)[:J]),
    }


def reference(tab_words, tab_scales, ws_words, ws_scales, wt_words, wt_scales, wd_words, wd_scales, b, wgo, offs, offs2):
    idx = unstriped(offs)
    idx2 = unstriped(offs2)
    tab_ = unpack_weight(tab_words, tab_scales, "e4m3")[:, idx]
    tabb_ = unpack_weight(tab_words, tab_scales, "e4m3")[:, idx2]
    ws_ = unpack_weight(ws_words, ws_scales, "e2m1")
    wt_ = unpack_weight(wt_words, wt_scales, "e4m3")
    a = ws_.T @ tab_ + wt_.T @ tabb_
    h = np.maximum(a, 0.0)
    h_ = mxq(h, 0, "e4m3")
    wd_ = unpack_weight(wd_words, wd_scales, "e4m3")
    y = wd_.T @ h_
    out = np.zeros((N, T))
    out[:, idx2] = f64(wgo)[0] * (y + f64(b)[:, None])
    return out

@@ -1,0 +1,205 @@
+from contextlib import ExitStack
+
+import concourse.mybir as mybir
+from concourse.masks import make_identity
+
+K, R, N, T, J = 1024, 512, 512, 2048, 1024
+FLOPS = 2 * (2 * K * R * J + R * N * J)
+
+F32 = mybir.dt.float32
+BF16 = mybir.dt.bfloat16
+I32 = mybir.dt.int32
+U32 = mybir.dt.uint32
+U16 = mybir.dt.uint16
+U8 = mybir.dt.uint8
+FP8X4 = mybir.dt.float8_e4m3fn_x4
+FP4X4 = mybir.dt.float4_e2m1fn_x4
+ACT = mybir.ActivationFunctionType
+MULT = mybir.AluOpType.mult
+
+P = 128
+HALF = J // 2
+TILES = HALF // P
+LIST_COLS = HALF // 16
+
+
+def tile_list_msg_relu_bias_kernel(
+    tc, tab_words, tab_scales, ws_words, ws_scales, wt_words, wt_scales, wd_words, wd_scales, b, wgo, offs, offs2, out
+):
+    nc = tc.nc
+    with ExitStack() as ctx:
+        keep = ctx.enter_context(tc.tile_pool(name="keep", bufs=1))
+        psum = ctx.enter_context(tc.psum_pool(name="psum", bufs=1))
+
+        src_list = keep.tile([P, J // 16], U16, name="src_list")
+        dst_list = keep.tile([P, J // 16], U16, name="dst_list")
+        tab0 = keep.tile([P, T], I32, name="tab0", tag="tab0", align_bytes=64)
+        tab1 = keep.tile([P, T], I32, name="tab1", align_bytes=64)
+        tab_sc = keep.tile([P, T], U8, name="tab_sc", tag="tab_sc", align_bytes=64)
+        ws = keep.tile([P, 2 * 2 * R], U8, name="ws", align_bytes=64)
+        wt = keep.tile([P, 2 * R], U32, name="wt", align_bytes=64)
+        w_sc = keep.tile([P, 3 * R], U8, name="w_sc", align_bytes=64)
+        src_sc = keep.tile([P, J], U8, name="src_sc", align_bytes=64)
+        src_sc1 = keep.tile([P, J], U8, name="src_sc1", align_bytes=64)
+        bias = keep.tile([P, N // P], F32, name="bias")
+        ident = keep.tile([P, P], F32, name="ident")
+        pages = [keep.tile([P, T], F32, name="page%d" % i) for i in range(3)]
+        acc = [psum.tile([P, R], F32, name="acc%d" % i) for i in range(TILES)]
+        ybank = [psum.tile([P, HALF], F32, name="ybank%d" % i) for i in range(4)]
+
+        nc.vector.memset(tab_sc[:].bitcast(I32), 0)
+        nc.vector.memset(w_sc[:].bitcast(I32), 0)
+        nc.vector.memset(src_sc1[:].bitcast(I32), 0)
+        for page in pages:
+            nc.vector.memset(page[:], 0.0)
+        make_identity(nc, ident[:])
+
+        def words(ap):
+            return ap.rearrange("p t i -> p (t i)").bitcast(I32)
+
+        nc.sync.dma_start(src_list[:], offs)
+        nc.sync.dma_start(tab0[:], words(tab_words[0]))
+        nc.sync.dma_start(dst_list[:], offs2)
+        for q in range(4):
+            nc.scalar.dma_start(
+                tab_sc[32 * q : 32 * q + 8, :].bitcast(I32), tab_scales[:, 4 * q : 4 * q + 4, :].bitcast(I32)
+            )
+        nc.sync.dma_start(
+            ws[:].bitcast(I32).rearrange("p (a w) -> p a w", a=2), ws_words.bitcast(I32).rearrange("a p w -> p a w")
+        )
+        nc.sync.dma_start(
+            wt[:].bitcast(I32).rearrange("p (a w) -> p a w", a=2),
+            wt_words.rearrange("a p r i -> a p (r i)").bitcast(I32).rearrange("a p w -> p a w"),
+        )
+        nc.sync.dma_start(tab1[:], words(tab_words[1]))
+        for first, scales in ((0, ws_scales), (4, wt_scales)):
+            for q in range(4):
+                rows = slice(32 * q + first, 32 * q + first + 4)
+                nc.scalar.dma_start(
+                    w_sc[rows, 0 : 2 * R].bitcast(I32).rearrange("p (a w) -> p a w", a=2),
+                    scales[:, 4 * q : 4 * q + 4, :].bitcast(I32).rearrange("a r w -> r a w"),
+                )
+        for q in range(4):
+            nc.scalar.dma_start(
+                w_sc[32 * q : 32 * q + 4, 2 * R : 3 * R].bitcast(I32), wd_scales[0, 4 * q : 4 * q + 4, :].bitcast(I32)
+            )
+        with nc.allow_non_contiguous_dma(reason="one bias value a partition"):
+            nc.gpsimd.dma_start(bias[:], b.rearrange("(m p) -> p m", p=P))
+
+        def gather_words(tab, lst, c, tag):
+            picked = keep.tile([P, HALF], U32, name="picked_" + tag, tag=tag, align_bytes=64)
+            nc.vector.tensor_copy(
+                picked[:], tab[:].bitcast(U32).indirect(lst[:, c * LIST_COLS : (c + 1) * LIST_COLS])
+            )
+            return picked
+
+        def gather_dst_scales(c):
+            picked = keep.tile([P, HALF], U8, name="dst_sc", tag="dst_sc", align_bytes=64)
+            nc.vector.tensor_copy(picked[:], tab_sc[:].indirect(dst_list[:, c * LIST_COLS : (c + 1) * LIST_COLS]))
+            return picked
+
+        def first_stage(c, s0, d0, d1, s1, dst_sc):
+            edges = c * HALF
+            passes = (
+                (s0, src_sc, 0, edges, ws[:, 0 : 2 * R].bitcast(FP4X4), w_sc[:, 0:R]),
+                (d0, dst_sc, 0, 0, wt[:, 0:R].bitcast(FP8X4), w_sc[4:P, 0:R]),
+                (d1, dst_sc, 4, 0, wt[:, R : 2 * R].bitcast(FP8X4), w_sc[4:P, R : 2 * R]),
+                (s1, src_sc1, 0, edges, ws[:, 2 * R : 4 * R].bitcast(FP4X4), w_sc[:, R : 2 * R]),
+            )
+            for i, (picked, plane, row, col, w, w_plane) in enumerate(passes):
+                for jt in range(TILES):
+                    nc.tensor.matmul_mx(
+                        acc[jt][:],
+                        lhsT=picked[:, jt * P : (jt + 1) * P].bitcast(FP8X4),
+                        lhsT_scale=plane[row:P, col + jt * P : col + (jt + 1) * P],
+                        rhs=w,
+                        rhs_scale=w_plane,
+                        start=(i == 0),
+                        stop=(i == len(passes) - 1),
+                    )
+
+        def hidden(c, tag):
+            relu = [keep.tile([P, R], BF16, name="relu%d" % jt, tag="relu%d" % jt) for jt in range(TILES)]
+            h = keep.tile([P, 4 * HALF], BF16, name="h_" + tag, tag=tag, align_bytes=64)
+            for jt in range(TILES):
+                nc.scalar.activation(
+                    relu[jt][:].rearrange("j (u p e) -> j u p e", u=2, e=2),
+                    acc[jt][:].rearrange("j (p u e) -> j u p e", u=2, e=2),
+                    ACT.Relu,
+                )
+            for jt in range(TILES):
+                pairs = relu[jt][:].bitcast(F32)
+                for u in range(2):
+                    nc.tensor.transpose(acc[jt][:, u * P : (u + 1) * P], pairs[:, u * P : (u + 1) * P], ident[:])
+            h_pairs = h[:].bitcast(F32)
+            for jt in range(TILES):
+                nc.scalar.copy(
+                    h_pairs[:, 2 * P * jt : 2 * P * (jt + 1)].rearrange("p (j u) -> p j u", u=2),
+                    acc[jt][:, 0 : 2 * P].rearrange("p (u j) -> p j u", u=2),
+                )
+            codes = keep.tile([P, HALF], U32, name="h_codes%d" % c, align_bytes=64)
+            plane = keep.tile([P, HALF], U8, name="h_plane%d" % c, align_bytes=64)
+            nc.vector.quantize_mx(out=codes[:].bitcast(FP8X4), scales=plane[:], in_=h[:])
+            return codes, plane
+
+        def message(m, hq, bank, y):
+            codes, plane = hq
+            nc.tensor.matmul_mx(
+                bank[:],
+                lhsT=wd[:, m * P : (m + 1) * P].bitcast(FP8X4),
+                lhsT_scale=w_sc[:, 2 * R + m * P : 2 * R + (m + 1) * P],
+                rhs=codes[:].bitcast(FP8X4),
+                rhs_scale=plane[:],
+                start=True,
+                stop=True,
+            )
+            nc.scalar.activation(y, bank[:], ACT.Identity, bias=bias[:, m : m + 1])
+
+        def place(m, c, hq, bank, page):
+            y = keep.tile([P, HALF], F32, name="y%d_%d" % (m, c))
+            message(m, hq, bank, y[:])
+            nc.vector.tensor_tensor(
+                page[:].indirect(dst_list[:, c * LIST_COLS : (c + 1) * LIST_COLS]),
+                y[:],
+                weight[:, c * HALF : (c + 1) * HALF],
+                MULT,
+            )
+
+        def store(m, page):
+            nc.sync.dma_start(out[m * P : (m + 1) * P, :], page[:])
+
+        s0 = gather_words(tab0, src_list, 0, "s0")
+        d0 = gather_words(tab0, dst_list, 0, "d0")
+        nc.vector.tensor_copy(src_sc[:], tab_sc[:].indirect(src_list[:]))
+        nc.gpsimd.dma_start(src_sc1[0:100, :].bitcast(I32), src_sc[4:104, :].bitcast(I32))
+        dst_sc = gather_dst_scales(0)
+        d1 = gather_words(tab1, dst_list, 0, "d1")
+        s1 = gather_words(tab1, src_list, 0, "s1")
+        first_stage(0, s0, d0, d1, s1, dst_sc)
+
+        s0 = gather_words(tab0, src_list, 1, "s0")
+        d0 = gather_words(tab0, dst_list, 1, "d0")
+        dst_sc = gather_dst_scales(1)
+        d1 = gather_words(tab1, dst_list, 1, "d1")
+
+        wd = keep.tile([P, N], U32, name="wd", tag="tab_sc", align_bytes=64)
+        nc.sync.dma_start(wd[:].bitcast(I32), words(wd_words[0]))
+        weight = keep.tile([P, J], F32, name="weight", tag="tab0", align_bytes=64)
+        nc.sync.dma_start(weight[:], wgo)
+
+        hq0 = hidden(0, "h0")
+        s1 = gather_words(tab1, src_list, 1, "h0")
+        place(0, 0, hq0, ybank[0], pages[0])
+        place(1, 0, hq0, ybank[1], pages[1])
+
+        first_stage(1, s0, d0, d1, s1, dst_sc)
+        hq1 = hidden(1, "h1")
+        place(2, 0, hq0, acc[TILES - 1], pages[2])
+        for m in range(3):
+            place(m, 1, hq1, ybank[(m + 2) % 4], pages[m])
+            store(m, pages[m])
+        y_last = keep.tile([P, J], F32, name="y_last")
+        message(3, hq0, ybank[1], y_last[:, 0:HALF])
+        message(3, hq1, ybank[2], y_last[:, HALF:J])
+        nc.vector.tensor_tensor(pages[0][:].indirect(dst_list[:]), y_last[:], weight[:], MULT)
+        store(3, pages[0])

@@ -34,36 +34,39 @@ def tile_list_msg_relu_bias_kernel(
         src_list = keep.tile([P, J // 16], U16, name="src_list")
         dst_list = keep.tile([P, J // 16], U16, name="dst_list")
         tab0 = keep.tile([P, T], I32, name="tab0", tag="tab0", align_bytes=64)
-        tab1 = keep.tile([P, T], I32, name="tab1", align_bytes=64)
+        tab1 = keep.tile([P, T], I32, name="tab1", tag="tab1", align_bytes=64)
         tab_sc = keep.tile([P, T], U8, name="tab_sc", tag="tab_sc", align_bytes=64)
         ws = keep.tile([P, 2 * 2 * R], U8, name="ws", align_bytes=64)
         wt = keep.tile([P, 2 * R], U32, name="wt", align_bytes=64)
         w_sc = keep.tile([P, 3 * R], U8, name="w_sc", align_bytes=64)
         src_sc = keep.tile([P, J], U8, name="src_sc", align_bytes=64)
         src_sc1 = keep.tile([P, J], U8, name="src_sc1", align_bytes=64)
+        wd = keep.tile([P, N], U32, name="wd", align_bytes=64)
+        weight = keep.tile([P, J], F32, name="weight")
         bias = keep.tile([P, N // P], F32, name="bias")
         ident = keep.tile([P, P], F32, name="ident")
-        pages = [keep.tile([P, T], F32, name="page%d" % i) for i in range(3)]
+        page0 = keep.tile([P, T], F32, name="page0")
         acc = [psum.tile([P, R], F32, name="acc%d" % i) for i in range(TILES)]
         ybank = [psum.tile([P, HALF], F32, name="ybank%d" % i) for i in range(4)]
 
         nc.vector.memset(tab_sc[:].bitcast(I32), 0)
         nc.vector.memset(w_sc[:].bitcast(I32), 0)
         nc.vector.memset(src_sc1[:].bitcast(I32), 0)
-        for page in pages:
-            nc.vector.memset(page[:], 0.0)
+        nc.vector.memset(page0[:], 0.0)
         make_identity(nc, ident[:])
 
         def words(ap):
             return ap.rearrange("p t i -> p (t i)").bitcast(I32)
 
         nc.sync.dma_start(src_list[:], offs)
-        nc.sync.dma_start(tab0[:], words(tab_words[0]))
         nc.sync.dma_start(dst_list[:], offs2)
         for q in range(4):
-            nc.scalar.dma_start(
+            queue = nc.scalar if q < 2 else nc.sync
+            queue.dma_start(
                 tab_sc[32 * q : 32 * q + 8, :].bitcast(I32), tab_scales[:, 4 * q : 4 * q + 4, :].bitcast(I32)
             )
+        nc.sync.dma_start(tab0[:], words(tab_words[0]))
+        nc.sync.dma_start(tab1[:], words(tab_words[1]))
         nc.sync.dma_start(
             ws[:].bitcast(I32).rearrange("p (a w) -> p a w", a=2), ws_words.bitcast(I32).rearrange("a p w -> p a w")
         )
@@ -71,7 +74,6 @@ def tile_list_msg_relu_bias_kernel(
             wt[:].bitcast(I32).rearrange("p (a w) -> p a w", a=2),
             wt_words.rearrange("a p r i -> a p (r i)").bitcast(I32).rearrange("a p w -> p a w"),
         )
-        nc.sync.dma_start(tab1[:], words(tab_words[1]))
         for first, scales in ((0, ws_scales), (4, wt_scales)):
             for q in range(4):
                 rows = slice(32 * q + first, 32 * q + first + 4)
@@ -83,8 +85,10 @@ def tile_list_msg_relu_bias_kernel(
             nc.scalar.dma_start(
                 w_sc[32 * q : 32 * q + 4, 2 * R : 3 * R].bitcast(I32), wd_scales[0, 4 * q : 4 * q + 4, :].bitcast(I32)
             )
+        nc.sync.dma_start(wd[:].bitcast(I32), words(wd_words[0]))
+        nc.sync.dma_start(weight[:], wgo)
         with nc.allow_non_contiguous_dma(reason="one bias value a partition"):
-            nc.gpsimd.dma_start(bias[:], b.rearrange("(m p) -> p m", p=P))
+            nc.sync.dma_start(bias[:], b.rearrange("(m p) -> p m", p=P))
 
         def gather_words(tab, lst, c, tag):
             picked = keep.tile([P, HALF], U32, name="picked_" + tag, tag=tag, align_bytes=64)
@@ -106,17 +110,19 @@ def tile_list_msg_relu_bias_kernel(
                 (d1, dst_sc, 4, 0, wt[:, R : 2 * R].bitcast(FP8X4), w_sc[4:P, R : 2 * R]),
                 (s1, src_sc1, 0, edges, ws[:, 2 * R : 4 * R].bitcast(FP4X4), w_sc[:, R : 2 * R]),
             )
-            for i, (picked, plane, row, col, w, w_plane) in enumerate(passes):
-                for jt in range(TILES):
-                    nc.tensor.matmul_mx(
-                        acc[jt][:],
-                        lhsT=picked[:, jt * P : (jt + 1) * P].bitcast(FP8X4),
-                        lhsT_scale=plane[row:P, col + jt * P : col + (jt + 1) * P],
-                        rhs=w,
-                        rhs_scale=w_plane,
-                        start=(i == 0),
-                        stop=(i == len(passes) - 1),
-                    )
+            order = [(i, jt) for i in (0, 1) for jt in range(TILES)]
+            order = order + [(i, jt) for jt in range(TILES) for i in (2, 3)]
+            for i, jt in order:
+                picked, plane, row, col, w, w_plane = passes[i]
+                nc.tensor.matmul_mx(
+                    acc[jt][:],
+                    lhsT=picked[:, jt * P : (jt + 1) * P].bitcast(FP8X4),
+                    lhsT_scale=plane[row:P, col + jt * P : col + (jt + 1) * P],
+                    rhs=w,
+                    rhs_scale=w_plane,
+                    start=(i == 0),
+                    stop=(i == len(passes) - 1),
+                )
 
         def hidden(c, tag):
             relu = [keep.tile([P, R], BF16, name="relu%d" % jt, tag="relu%d" % jt) for jt in range(TILES)]
@@ -168,11 +174,11 @@ def tile_list_msg_relu_bias_kernel(
         def store(m, page):
             nc.sync.dma_start(out[m * P : (m + 1) * P, :], page[:])
 
-        s0 = gather_words(tab0, src_list, 0, "s0")
-        d0 = gather_words(tab0, dst_list, 0, "d0")
         nc.vector.tensor_copy(src_sc[:], tab_sc[:].indirect(src_list[:]))
         nc.gpsimd.dma_start(src_sc1[0:100, :].bitcast(I32), src_sc[4:104, :].bitcast(I32))
         dst_sc = gather_dst_scales(0)
+        s0 = gather_words(tab0, src_list, 0, "s0")
+        d0 = gather_words(tab0, dst_list, 0, "d0")
         d1 = gather_words(tab1, dst_list, 0, "d1")
         s1 = gather_words(tab1, src_list, 0, "s1")
         first_stage(0, s0, d0, d1, s1, dst_sc)
@@ -182,17 +188,17 @@ def tile_list_msg_relu_bias_kernel(
         dst_sc = gather_dst_scales(1)
         d1 = gather_words(tab1, dst_list, 1, "d1")
 
-        wd = keep.tile([P, N], U32, name="wd", tag="tab_sc", align_bytes=64)
-        nc.sync.dma_start(wd[:].bitcast(I32), words(wd_words[0]))
-        weight = keep.tile([P, J], F32, name="weight", tag="tab0", align_bytes=64)
-        nc.sync.dma_start(weight[:], wgo)
-
         hq0 = hidden(0, "h0")
         s1 = gather_words(tab1, src_list, 1, "h0")
-        place(0, 0, hq0, ybank[0], pages[0])
-        place(1, 0, hq0, ybank[1], pages[1])
+        page1 = keep.tile([P, T], F32, name="page1", tag="tab1", align_bytes=64)
+        nc.gpsimd.memset(page1[:], 0.0)
+        place(0, 0, hq0, ybank[0], page0)
+        place(1, 0, hq0, ybank[1], page1)
 
         first_stage(1, s0, d0, d1, s1, dst_sc)
+        page2 = keep.tile([P, T], F32, name="page2", tag="h0", align_bytes=64)
+        nc.gpsimd.memset(page2[:], 0.0)
+        pages = (page0, page1, page2)
         hq1 = hidden(1, "h1")
         place(2, 0, hq0, acc[TILES - 1], pages[2])
         for m in range(3):

@@ -38,7 +38,7 @@ def tile_list_msg_relu_bias_kernel(
         tab_sc = keep.tile([P, T], U8, name="tab_sc", tag="tab_sc", align_bytes=64)
         ws = keep.tile([P, 2 * 2 * R], U8, name="ws", align_bytes=64)
         wt = keep.tile([P, 2 * R], U32, name="wt", align_bytes=64)
-        w_sc = keep.tile([P, 3 * R], U8, name="w_sc", align_bytes=64)
+        w_sc = keep.tile([P, 5 * R], U8, name="w_sc", align_bytes=64)
         src_sc = keep.tile([P, J], U8, name="src_sc", align_bytes=64)
         src_sc1 = keep.tile([P, J], U8, name="src_sc1", align_bytes=64)
         wd = keep.tile([P, N], U32, name="wd", align_bytes=64)
@@ -52,7 +52,7 @@ def tile_list_msg_relu_bias_kernel(
         nc.vector.memset(tab_sc[:].bitcast(I32), 0)
         nc.vector.memset(w_sc[:].bitcast(I32), 0)
         nc.vector.memset(src_sc1[:].bitcast(I32), 0)
-        nc.vector.memset(page0[:], 0.0)
+        nc.vector.memset(page0[:].bitcast(I32), 0)
         make_identity(nc, ident[:])
 
         def words(ap):
@@ -61,34 +61,29 @@ def tile_list_msg_relu_bias_kernel(
         nc.sync.dma_start(src_list[:], offs)
         nc.sync.dma_start(dst_list[:], offs2)
         for q in range(4):
-            queue = nc.scalar if q < 2 else nc.sync
-            queue.dma_start(
+            nc.sync.dma_start(
                 tab_sc[32 * q : 32 * q + 8, :].bitcast(I32), tab_scales[:, 4 * q : 4 * q + 4, :].bitcast(I32)
             )
         nc.sync.dma_start(tab0[:], words(tab_words[0]))
         nc.sync.dma_start(tab1[:], words(tab_words[1]))
+
+        def load_planes(scales, col):
+            passes = scales.shape[0]
+            for q in range(4):
+                nc.sync.dma_start(
+                    w_sc[32 * q : 32 * q + 4, col : col + passes * R].bitcast(I32).rearrange("p (a w) -> p a w", a=passes),
+                    scales[:, 4 * q : 4 * q + 4, :].bitcast(I32).rearrange("a r w -> r a w"),
+                )
+
         nc.sync.dma_start(
             ws[:].bitcast(I32).rearrange("p (a w) -> p a w", a=2), ws_words.bitcast(I32).rearrange("a p w -> p a w")
         )
+        load_planes(ws_scales, 0)
         nc.sync.dma_start(
             wt[:].bitcast(I32).rearrange("p (a w) -> p a w", a=2),
             wt_words.rearrange("a p r i -> a p (r i)").bitcast(I32).rearrange("a p w -> p a w"),
         )
-        for first, scales in ((0, ws_scales), (4, wt_scales)):
-            for q in range(4):
-                rows = slice(32 * q + first, 32 * q + first + 4)
-                nc.scalar.dma_start(
-                    w_sc[rows, 0 : 2 * R].bitcast(I32).rearrange("p (a w) -> p a w", a=2),
-                    scales[:, 4 * q : 4 * q + 4, :].bitcast(I32).rearrange("a r w -> r a w"),
-                )
-        for q in range(4):
-            nc.scalar.dma_start(
-                w_sc[32 * q : 32 * q + 4, 2 * R : 3 * R].bitcast(I32), wd_scales[0, 4 * q : 4 * q + 4, :].bitcast(I32)
-            )
-        nc.sync.dma_start(wd[:].bitcast(I32), words(wd_words[0]))
-        nc.sync.dma_start(weight[:], wgo)
-        with nc.allow_non_contiguous_dma(reason="one bias value a partition"):
-            nc.sync.dma_start(bias[:], b.rearrange("(m p) -> p m", p=P))
+        load_planes(wt_scales, 2 * R)
 
         def gather_words(tab, lst, c, tag):
             picked = keep.tile([P, HALF], U32, name="picked_" + tag, tag=tag, align_bytes=64)
@@ -106,8 +101,8 @@ def tile_list_msg_relu_bias_kernel(
             edges = c * HALF
             passes = (
                 (s0, src_sc, 0, edges, ws[:, 0 : 2 * R].bitcast(FP4X4), w_sc[:, 0:R]),
-                (d0, dst_sc, 0, 0, wt[:, 0:R].bitcast(FP8X4), w_sc[4:P, 0:R]),
-                (d1, dst_sc, 4, 0, wt[:, R : 2 * R].bitcast(FP8X4), w_sc[4:P, R : 2 * R]),
+                (d0, dst_sc, 0, 0, wt[:, 0:R].bitcast(FP8X4), w_sc[:, 2 * R : 3 * R]),
+                (d1, dst_sc, 4, 0, wt[:, R : 2 * R].bitcast(FP8X4), w_sc[:, 3 * R : 4 * R]),
                 (s1, src_sc1, 0, edges, ws[:, 2 * R : 4 * R].bitcast(FP4X4), w_sc[:, R : 2 * R]),
             )
             order = [(i, jt) for i in (0, 1) for jt in range(TILES)]
@@ -153,7 +148,7 @@ def tile_list_msg_relu_bias_kernel(
             nc.tensor.matmul_mx(
                 bank[:],
                 lhsT=wd[:, m * P : (m + 1) * P].bitcast(FP8X4),
-                lhsT_scale=w_sc[:, 2 * R + m * P : 2 * R + (m + 1) * P],
+                lhsT_scale=w_sc[:, 4 * R + m * P : 4 * R + (m + 1) * P],
                 rhs=codes[:].bitcast(FP8X4),
                 rhs_scale=plane[:],
                 start=True,
@@ -175,7 +170,15 @@ def tile_list_msg_relu_bias_kernel(
             nc.sync.dma_start(out[m * P : (m + 1) * P, :], page[:])
 
         nc.vector.tensor_copy(src_sc[:], tab_sc[:].indirect(src_list[:]))
-        nc.gpsimd.dma_start(src_sc1[0:100, :].bitcast(I32), src_sc[4:104, :].bitcast(I32))
+        for q in range(4):
+            nc.sync.dma_start(
+                src_sc1[32 * q : 32 * q + 4, :].bitcast(I32), src_sc[32 * q + 4 : 32 * q + 8, :].bitcast(I32)
+            )
+        nc.sync.dma_start(wd[:].bitcast(I32), words(wd_words[0]))
+        load_planes(wd_scales, 4 * R)
+        nc.sync.dma_start(weight[:], wgo)
+        with nc.allow_non_contiguous_dma(reason="one bias value a partition"):
+            nc.sync.dma_start(bias[:], b.rearrange("(m p) -> p m", p=P))
         dst_sc = gather_dst_scales(0)
         s0 = gather_words(tab0, src_list, 0, "s0")
         d0 = gather_words(tab0, dst_list, 0, "d0")

@@ -33,9 +33,9 @@ def tile_list_msg_relu_bias_kernel(
 
         src_list = keep.tile([P, J // 16], U16, name="src_list")
         dst_list = keep.tile([P, J // 16], U16, name="dst_list")
-        tab0 = keep.tile([P, T], I32, name="tab0", tag="tab0", align_bytes=64)
-        tab1 = keep.tile([P, T], I32, name="tab1", tag="tab1", align_bytes=64)
-        tab_sc = keep.tile([P, T], U8, name="tab_sc", tag="tab_sc", align_bytes=64)
+        tab0 = keep.tile([P, T], I32, name="tab0", align_bytes=64)
+        tab1 = keep.tile([P, T], I32, name="tab1", align_bytes=64)
+        tab_sc = keep.tile([P, T], U8, name="tab_sc", align_bytes=64)
         ws = keep.tile([P, 2 * 2 * R], U8, name="ws", align_bytes=64)
         wt = keep.tile([P, 2 * R], U32, name="wt", align_bytes=64)
         w_sc = keep.tile([P, 5 * R], U8, name="w_sc", align_bytes=64)
@@ -45,27 +45,19 @@ def tile_list_msg_relu_bias_kernel(
         weight = keep.tile([P, J], F32, name="weight")
         bias = keep.tile([P, N // P], F32, name="bias")
         ident = keep.tile([P, P], F32, name="ident")
-        page0 = keep.tile([P, T], F32, name="page0")
-        acc = [psum.tile([P, R], F32, name="acc%d" % i) for i in range(TILES)]
-        ybank = [psum.tile([P, HALF], F32, name="ybank%d" % i) for i in range(4)]
+        page_a = keep.tile([P, T], F32, name="page_a")
+        page_b = keep.tile([P, T], F32, name="page_b")
+        bank = [psum.tile([P, R], F32, name="bank%d" % i) for i in range(8)]
 
         nc.vector.memset(tab_sc[:].bitcast(I32), 0)
         nc.vector.memset(w_sc[:].bitcast(I32), 0)
         nc.vector.memset(src_sc1[:].bitcast(I32), 0)
-        nc.vector.memset(page0[:].bitcast(I32), 0)
+        nc.vector.memset(page_a[:].bitcast(I32), 0)
+        nc.vector.memset(page_b[:].bitcast(I32), 0)
         make_identity(nc, ident[:])
 
         def words(ap):
             return ap.rearrange("p t i -> p (t i)").bitcast(I32)
-
-        nc.sync.dma_start(src_list[:], offs)
-        nc.sync.dma_start(dst_list[:], offs2)
-        for q in range(4):
-            nc.sync.dma_start(
-                tab_sc[32 * q : 32 * q + 8, :].bitcast(I32), tab_scales[:, 4 * q : 4 * q + 4, :].bitcast(I32)
-            )
-        nc.sync.dma_start(tab0[:], words(tab_words[0]))
-        nc.sync.dma_start(tab1[:], words(tab_words[1]))
 
         def load_planes(scales, col):
             passes = scales.shape[0]
@@ -75,78 +67,89 @@ def tile_list_msg_relu_bias_kernel(
                     scales[:, 4 * q : 4 * q + 4, :].bitcast(I32).rearrange("a r w -> r a w"),
                 )
 
+        nc.sync.dma_start(src_list[:], offs)
+        nc.sync.dma_start(tab0[:], words(tab_words[0]))
+        for q in range(4):
+            nc.sync.dma_start(
+                tab_sc[32 * q : 32 * q + 8, :].bitcast(I32), tab_scales[:, 4 * q : 4 * q + 4, :].bitcast(I32)
+            )
+        nc.sync.dma_start(dst_list[:], offs2)
         nc.sync.dma_start(
             ws[:].bitcast(I32).rearrange("p (a w) -> p a w", a=2), ws_words.bitcast(I32).rearrange("a p w -> p a w")
         )
-        load_planes(ws_scales, 0)
         nc.sync.dma_start(
             wt[:].bitcast(I32).rearrange("p (a w) -> p a w", a=2),
             wt_words.rearrange("a p r i -> a p (r i)").bitcast(I32).rearrange("a p w -> p a w"),
         )
+        load_planes(ws_scales, 0)
+        nc.sync.dma_start(tab1[:], words(tab_words[1]))
         load_planes(wt_scales, 2 * R)
 
-        def gather_words(tab, lst, c, tag):
-            picked = keep.tile([P, HALF], U32, name="picked_" + tag, tag=tag, align_bytes=64)
-            nc.vector.tensor_copy(
-                picked[:], tab[:].bitcast(U32).indirect(lst[:, c * LIST_COLS : (c + 1) * LIST_COLS])
-            )
+        def entries(lst, lo, hi):
+            return lst[:, lo // 16 : hi // 16]
+
+        def gather_words(picked, tab, lst, lo, hi):
+            nc.vector.tensor_copy(picked, tab[:].bitcast(U32).indirect(entries(lst, lo, hi)))
+
+        def word_tile(name, tag, width):
+            return keep.tile([P, width], U32, name=name, tag=tag, align_bytes=64)
+
+        def gather_dst_scales(c, tag):
+            picked = keep.tile([P, HALF], U8, name="dst_sc%d" % c, tag=tag, align_bytes=64)
+            nc.vector.tensor_copy(picked[:], tab_sc[:].indirect(entries(dst_list, c * HALF, (c + 1) * HALF)))
             return picked
 
-        def gather_dst_scales(c):
-            picked = keep.tile([P, HALF], U8, name="dst_sc", tag="dst_sc", align_bytes=64)
-            nc.vector.tensor_copy(picked[:], tab_sc[:].indirect(dst_list[:, c * LIST_COLS : (c + 1) * LIST_COLS]))
-            return picked
-
-        def first_stage(c, s0, d0, d1, s1, dst_sc):
-            edges = c * HALF
-            passes = (
-                (s0, src_sc, 0, edges, ws[:, 0 : 2 * R].bitcast(FP4X4), w_sc[:, 0:R]),
-                (d0, dst_sc, 0, 0, wt[:, 0:R].bitcast(FP8X4), w_sc[:, 2 * R : 3 * R]),
-                (d1, dst_sc, 4, 0, wt[:, R : 2 * R].bitcast(FP8X4), w_sc[:, 3 * R : 4 * R]),
-                (s1, src_sc1, 0, edges, ws[:, 2 * R : 4 * R].bitcast(FP4X4), w_sc[:, R : 2 * R]),
+        def mx_pass(c, jt, i, picked, dst_sc):
+            plane, row, col, w, w_plane = (
+                (src_sc, 0, c * HALF, ws[:, 0 : 2 * R].bitcast(FP4X4), w_sc[:, 0:R]),
+                (dst_sc, 0, 0, wt[:, 0:R].bitcast(FP8X4), w_sc[:, 2 * R : 3 * R]),
+                (dst_sc, 4, 0, wt[:, R : 2 * R].bitcast(FP8X4), w_sc[:, 3 * R : 4 * R]),
+                (src_sc1, 0, c * HALF, ws[:, 2 * R : 4 * R].bitcast(FP4X4), w_sc[:, R : 2 * R]),
+            )[i]
+            nc.tensor.matmul_mx(
+                bank[4 * c + jt][:],
+                lhsT=picked.bitcast(FP8X4),
+                lhsT_scale=plane[row:P, col + jt * P : col + (jt + 1) * P],
+                rhs=w,
+                rhs_scale=w_plane,
+                start=(i == 0),
+                stop=(i == 3),
             )
-            order = [(i, jt) for i in (0, 1) for jt in range(TILES)]
-            order = order + [(i, jt) for jt in range(TILES) for i in (2, 3)]
-            for i, jt in order:
-                picked, plane, row, col, w, w_plane = passes[i]
-                nc.tensor.matmul_mx(
-                    acc[jt][:],
-                    lhsT=picked[:, jt * P : (jt + 1) * P].bitcast(FP8X4),
-                    lhsT_scale=plane[row:P, col + jt * P : col + (jt + 1) * P],
-                    rhs=w,
-                    rhs_scale=w_plane,
-                    start=(i == 0),
-                    stop=(i == len(passes) - 1),
-                )
 
-        def hidden(c, tag):
-            relu = [keep.tile([P, R], BF16, name="relu%d" % jt, tag="relu%d" % jt) for jt in range(TILES)]
-            h = keep.tile([P, 4 * HALF], BF16, name="h_" + tag, tag=tag, align_bytes=64)
+        def cols(t, jt):
+            return t[:, jt * P : (jt + 1) * P]
+
+        def hidden(c, turn):
+            relu = [keep.tile([P, R], BF16, name="relu%d_%d" % (c, jt), tag="relu%d" % jt, align_bytes=64) for jt in range(TILES)]
+            h = keep.tile([P, 4 * HALF], BF16, name="h%d" % c, tag="h%d" % c, align_bytes=64)
             for jt in range(TILES):
                 nc.scalar.activation(
                     relu[jt][:].rearrange("j (u p e) -> j u p e", u=2, e=2),
-                    acc[jt][:].rearrange("j (p u e) -> j u p e", u=2, e=2),
+                    bank[4 * c + jt][:].rearrange("j (p u e) -> j u p e", u=2, e=2),
                     ACT.Relu,
                 )
             for jt in range(TILES):
                 pairs = relu[jt][:].bitcast(F32)
                 for u in range(2):
-                    nc.tensor.transpose(acc[jt][:, u * P : (u + 1) * P], pairs[:, u * P : (u + 1) * P], ident[:])
+                    nc.tensor.transpose(turn[jt][:, u * P : (u + 1) * P], pairs[:, u * P : (u + 1) * P], ident[:])
             h_pairs = h[:].bitcast(F32)
             for jt in range(TILES):
                 nc.scalar.copy(
                     h_pairs[:, 2 * P * jt : 2 * P * (jt + 1)].rearrange("p (j u) -> p j u", u=2),
-                    acc[jt][:, 0 : 2 * P].rearrange("p (u j) -> p j u", u=2),
+                    turn[jt][:, 0 : 2 * P].rearrange("p (u j) -> p j u", u=2),
                 )
+            return h
+
+        def quantise(c, h):
             codes = keep.tile([P, HALF], U32, name="h_codes%d" % c, align_bytes=64)
             plane = keep.tile([P, HALF], U8, name="h_plane%d" % c, align_bytes=64)
             nc.vector.quantize_mx(out=codes[:].bitcast(FP8X4), scales=plane[:], in_=h[:])
             return codes, plane
 
-        def message(m, hq, bank, y):
+        def product(m, hq, acc):
             codes, plane = hq
             nc.tensor.matmul_mx(
-                bank[:],
+                acc[:],
                 lhsT=wd[:, m * P : (m + 1) * P].bitcast(FP8X4),
                 lhsT_scale=w_sc[:, 4 * R + m * P : 4 * R + (m + 1) * P],
                 rhs=codes[:].bitcast(FP8X4),
@@ -154,61 +157,84 @@ def tile_list_msg_relu_bias_kernel(
                 start=True,
                 stop=True,
             )
-            nc.scalar.activation(y, bank[:], ACT.Identity, bias=bias[:, m : m + 1])
 
-        def place(m, c, hq, bank, page):
-            y = keep.tile([P, HALF], F32, name="y%d_%d" % (m, c))
-            message(m, hq, bank, y[:])
-            nc.vector.tensor_tensor(
-                page[:].indirect(dst_list[:, c * LIST_COLS : (c + 1) * LIST_COLS]),
-                y[:],
-                weight[:, c * HALF : (c + 1) * HALF],
-                MULT,
-            )
+        def add_bias(m, c, acc, y):
+            nc.scalar.activation(y[:, c * HALF : (c + 1) * HALF], acc[:], ACT.Identity, bias=bias[:, m : m + 1])
+
+        def place(page, y, lo, hi):
+            nc.vector.tensor_tensor(page[:].indirect(entries(dst_list, lo, hi)), y[:, lo:hi], weight[:, lo:hi], MULT)
 
         def store(m, page):
             nc.sync.dma_start(out[m * P : (m + 1) * P, :], page[:])
 
+        quarter = HALF // 2
+        s0 = word_tile("s0_0", "s0", HALF)
+        gather_words(s0[:], tab0, src_list, 0, HALF)
         nc.vector.tensor_copy(src_sc[:], tab_sc[:].indirect(src_list[:]))
-        for q in range(4):
-            nc.sync.dma_start(
-                src_sc1[32 * q : 32 * q + 4, :].bitcast(I32), src_sc[32 * q + 4 : 32 * q + 8, :].bitcast(I32)
-            )
+        nc.sync.dma_start(src_sc1[0 : P - 4, :].bitcast(I32), src_sc[4:P, :].bitcast(I32))
         nc.sync.dma_start(wd[:].bitcast(I32), words(wd_words[0]))
         load_planes(wd_scales, 4 * R)
         nc.sync.dma_start(weight[:], wgo)
         with nc.allow_non_contiguous_dma(reason="one bias value a partition"):
             nc.sync.dma_start(bias[:], b.rearrange("(m p) -> p m", p=P))
-        dst_sc = gather_dst_scales(0)
-        s0 = gather_words(tab0, src_list, 0, "s0")
-        d0 = gather_words(tab0, dst_list, 0, "d0")
-        d1 = gather_words(tab1, dst_list, 0, "d1")
-        s1 = gather_words(tab1, src_list, 0, "s1")
-        first_stage(0, s0, d0, d1, s1, dst_sc)
+        dst_sc = gather_dst_scales(0, "dst_sc")
+        d0 = word_tile("d0_0", "d0", HALF)
+        gather_words(d0[:], tab0, dst_list, 0, HALF)
+        d1, s1 = [], []
+        for g in range(2):
+            d1.append(word_tile("d1_%d" % g, "hold_s0" if g == 0 else "d1b", quarter))
+            gather_words(d1[g][:], tab1, dst_list, g * quarter, (g + 1) * quarter)
+            s1.append(word_tile("s1_%d" % g, "s1_%d" % g, quarter))
+            gather_words(s1[g][:], tab1, src_list, g * quarter, (g + 1) * quarter)
+        for i, picked in ((0, s0), (1, d0)):
+            for jt in range(TILES):
+                mx_pass(0, jt, i, cols(picked, jt), dst_sc)
+        for jt in range(TILES):
+            mx_pass(0, jt, 2, cols(d1[jt // 2], jt % 2), dst_sc)
+            mx_pass(0, jt, 3, cols(s1[jt // 2], jt % 2), dst_sc)
 
-        s0 = gather_words(tab0, src_list, 1, "s0")
-        d0 = gather_words(tab0, dst_list, 1, "d0")
-        dst_sc = gather_dst_scales(1)
-        d1 = gather_words(tab1, dst_list, 1, "d1")
+        s0 = word_tile("s0_1", "hold_s0", HALF)
+        gather_words(s0[:], tab0, src_list, HALF, J)
+        d0 = word_tile("d0_1", "d0", HALF)
+        gather_words(d0[:], tab0, dst_list, HALF, J)
+        h0 = hidden(0, bank[4:8])
+        dst_sc = gather_dst_scales(1, "dst_sc")
+        hq0 = quantise(0, h0)
+        late = word_tile("late", "h0", J)
+        for g in range(2):
+            gather_words(late[:, 2 * g * quarter : (2 * g + 1) * quarter], tab1, dst_list, HALF + g * quarter, HALF + (g + 1) * quarter)
+            gather_words(late[:, (2 * g + 1) * quarter : (2 * g + 2) * quarter], tab1, src_list, HALF + g * quarter, HALF + (g + 1) * quarter)
+        y0 = keep.tile([P, J], F32, name="y0")
+        product(0, hq0, bank[0])
+        add_bias(0, 0, bank[0], y0)
+        product(1, hq0, bank[1])
+        place(page_a, y0, 0, HALF)
 
-        hq0 = hidden(0, "h0")
-        s1 = gather_words(tab1, src_list, 1, "h0")
-        page1 = keep.tile([P, T], F32, name="page1", tag="tab1", align_bytes=64)
-        nc.gpsimd.memset(page1[:], 0.0)
-        place(0, 0, hq0, ybank[0], page0)
-        place(1, 0, hq0, ybank[1], page1)
+        for i, picked in ((0, s0), (1, d0)):
+            for jt in range(TILES):
+                mx_pass(1, jt, i, cols(picked, jt), dst_sc)
+        for jt in range(TILES):
+            mx_pass(1, jt, 2, cols(late, 4 * (jt // 2) + jt % 2), dst_sc)
+            mx_pass(1, jt, 3, cols(late, 4 * (jt // 2) + 2 + jt % 2), dst_sc)
+        hq1 = quantise(1, hidden(1, bank[4:8]))
 
-        first_stage(1, s0, d0, d1, s1, dst_sc)
-        page2 = keep.tile([P, T], F32, name="page2", tag="h0", align_bytes=64)
-        nc.gpsimd.memset(page2[:], 0.0)
-        pages = (page0, page1, page2)
-        hq1 = hidden(1, "h1")
-        place(2, 0, hq0, acc[TILES - 1], pages[2])
-        for m in range(3):
-            place(m, 1, hq1, ybank[(m + 2) % 4], pages[m])
-            store(m, pages[m])
-        y_last = keep.tile([P, J], F32, name="y_last")
-        message(3, hq0, ybank[1], y_last[:, 0:HALF])
-        message(3, hq1, ybank[2], y_last[:, HALF:J])
-        nc.vector.tensor_tensor(pages[0][:].indirect(dst_list[:]), y_last[:], weight[:], MULT)
-        store(3, pages[0])
+        y1 = keep.tile([P, J], F32, name="y1", tag="relu3", align_bytes=64)
+        add_bias(1, 0, bank[1], y1)
+        cover = 3 * P
+        place(page_b, y1, 0, cover)
+        product(0, hq1, bank[2])
+        add_bias(0, 1, bank[2], y0)
+        place(page_a, y0, HALF, J)
+        store(0, page_a)
+        product(1, hq1, bank[3])
+        add_bias(1, 1, bank[3], y1)
+        place(page_b, y1, cover, J)
+        store(1, page_b)
+        for m, page in ((2, page_a), (3, page_b)):
+            y = keep.tile([P, J], F32, name="y%d" % m)
+            product(m, hq0, bank[m + 4])
+            add_bias(m, 0, bank[m + 4], y)
+            product(m, hq1, bank[m + 2])
+            add_bias(m, 1, bank[m + 2], y)
+            place(page, y, 0, J)
+            store(m, page)

@@ -40,6 +40,7 @@ def tile_list_msg_relu_bias_kernel(
         wt = keep.tile([P, 2 * R], U32, name="wt", align_bytes=64)
         w_sc = keep.tile([P, 5 * R], U8, name="w_sc", align_bytes=64)
         src_sc = keep.tile([P, J], U8, name="src_sc", align_bytes=64)
+        dst_sc = keep.tile([P, J], U8, name="dst_sc", align_bytes=64)
         src_sc1 = keep.tile([P, J], U8, name="src_sc1", align_bytes=64)
         wd = keep.tile([P, N], U32, name="wd", align_bytes=64)
         weight = keep.tile([P, J], F32, name="weight")
@@ -68,22 +69,29 @@ def tile_list_msg_relu_bias_kernel(
                 )
 
         nc.sync.dma_start(src_list[:], offs)
-        nc.sync.dma_start(tab0[:], words(tab_words[0]))
+        nc.sync.dma_start(
+            ws[:].bitcast(I32).rearrange("p (a w) -> p a w", a=2), ws_words.bitcast(I32).rearrange("a p w -> p a w")
+        )
         for q in range(4):
             nc.sync.dma_start(
                 tab_sc[32 * q : 32 * q + 8, :].bitcast(I32), tab_scales[:, 4 * q : 4 * q + 4, :].bitcast(I32)
             )
+        nc.sync.dma_start(tab0[:], words(tab_words[0]))
         nc.sync.dma_start(dst_list[:], offs2)
-        nc.sync.dma_start(
-            ws[:].bitcast(I32).rearrange("p (a w) -> p a w", a=2), ws_words.bitcast(I32).rearrange("a p w -> p a w")
-        )
+        load_planes(ws_scales, 0)
         nc.sync.dma_start(
             wt[:].bitcast(I32).rearrange("p (a w) -> p a w", a=2),
             wt_words.rearrange("a p r i -> a p (r i)").bitcast(I32).rearrange("a p w -> p a w"),
         )
-        load_planes(ws_scales, 0)
         nc.sync.dma_start(tab1[:], words(tab_words[1]))
         load_planes(wt_scales, 2 * R)
+        nc.vector.tensor_copy(src_sc[:], tab_sc[:].indirect(src_list[:]))
+        nc.sync.dma_start(src_sc1[0 : P - 4, :].bitcast(I32), src_sc[4:P, :].bitcast(I32))
+        nc.sync.dma_start(wd[:].bitcast(I32), words(wd_words[0]))
+        load_planes(wd_scales, 4 * R)
+        with nc.allow_non_contiguous_dma(reason="one bias value a partition"):
+            nc.sync.dma_start(bias[:], b.rearrange("(m p) -> p m", p=P))
+        nc.sync.dma_start(weight[:], wgo)
 
         def entries(lst, lo, hi):
             return lst[:, lo // 16 : hi // 16]
@@ -94,22 +102,17 @@ def tile_list_msg_relu_bias_kernel(
         def word_tile(name, tag, width):
             return keep.tile([P, width], U32, name=name, tag=tag, align_bytes=64)
 
-        def gather_dst_scales(c, tag):
-            picked = keep.tile([P, HALF], U8, name="dst_sc%d" % c, tag=tag, align_bytes=64)
-            nc.vector.tensor_copy(picked[:], tab_sc[:].indirect(entries(dst_list, c * HALF, (c + 1) * HALF)))
-            return picked
-
-        def mx_pass(c, jt, i, picked, dst_sc):
-            plane, row, col, w, w_plane = (
-                (src_sc, 0, c * HALF, ws[:, 0 : 2 * R].bitcast(FP4X4), w_sc[:, 0:R]),
-                (dst_sc, 0, 0, wt[:, 0:R].bitcast(FP8X4), w_sc[:, 2 * R : 3 * R]),
-                (dst_sc, 4, 0, wt[:, R : 2 * R].bitcast(FP8X4), w_sc[:, 3 * R : 4 * R]),
-                (src_sc1, 0, c * HALF, ws[:, 2 * R : 4 * R].bitcast(FP4X4), w_sc[:, R : 2 * R]),
+        def mx_pass(jt, i, picked):
+            plane, row, w, w_plane = (
+                (src_sc, 0, ws[:, 0 : 2 * R].bitcast(FP4X4), w_sc[:, 0:R]),
+                (dst_sc, 0, wt[:, 0:R].bitcast(FP8X4), w_sc[:, 2 * R : 3 * R]),
+                (dst_sc, 4, wt[:, R : 2 * R].bitcast(FP8X4), w_sc[:, 3 * R : 4 * R]),
+                (src_sc1, 0, ws[:, 2 * R : 4 * R].bitcast(FP4X4), w_sc[:, R : 2 * R]),
             )[i]
             nc.tensor.matmul_mx(
-                bank[4 * c + jt][:],
+                bank[jt][:],
                 lhsT=picked.bitcast(FP8X4),
-                lhsT_scale=plane[row:P, col + jt * P : col + (jt + 1) * P],
+                lhsT_scale=plane[row:P, jt * P : (jt + 1) * P],
                 rhs=w,
                 rhs_scale=w_plane,
                 start=(i == 0),
@@ -119,37 +122,39 @@ def tile_list_msg_relu_bias_kernel(
         def cols(t, jt):
             return t[:, jt * P : (jt + 1) * P]
 
-        def hidden(c, turn):
-            relu = [keep.tile([P, R], BF16, name="relu%d_%d" % (c, jt), tag="relu%d" % jt, align_bytes=64) for jt in range(TILES)]
-            h = keep.tile([P, 4 * HALF], BF16, name="h%d" % c, tag="h%d" % c, align_bytes=64)
-            for jt in range(TILES):
+        def hidden(name, tiles):
+            relu = [keep.tile([P, R], BF16, name="relu%d" % jt, tag="relu%d" % jt, align_bytes=64) for jt in tiles]
+            h = keep.tile([P, 4 * P * len(tiles)], BF16, name=name, tag=name, align_bytes=64)
+            turn = [bank[TILES + jt % TILES] for jt in tiles]
+            for i, jt in enumerate(tiles):
                 nc.scalar.activation(
-                    relu[jt][:].rearrange("j (u p e) -> j u p e", u=2, e=2),
-                    bank[4 * c + jt][:].rearrange("j (p u e) -> j u p e", u=2, e=2),
+                    relu[i][:].rearrange("j (u p e) -> j u p e", u=2, e=2),
+                    bank[jt][:].rearrange("j (p u e) -> j u p e", u=2, e=2),
                     ACT.Relu,
                 )
-            for jt in range(TILES):
-                pairs = relu[jt][:].bitcast(F32)
+            for i in range(len(tiles)):
+                pairs = relu[i][:].bitcast(F32)
                 for u in range(2):
-                    nc.tensor.transpose(turn[jt][:, u * P : (u + 1) * P], pairs[:, u * P : (u + 1) * P], ident[:])
+                    nc.tensor.transpose(turn[i][:, u * P : (u + 1) * P], pairs[:, u * P : (u + 1) * P], ident[:])
             h_pairs = h[:].bitcast(F32)
-            for jt in range(TILES):
+            for i in range(len(tiles)):
                 nc.scalar.copy(
-                    h_pairs[:, 2 * P * jt : 2 * P * (jt + 1)].rearrange("p (j u) -> p j u", u=2),
-                    turn[jt][:, 0 : 2 * P].rearrange("p (u j) -> p j u", u=2),
+                    h_pairs[:, 2 * P * i : 2 * P * (i + 1)].rearrange("p (j u) -> p j u", u=2),
+                    turn[i][:, 0 : 2 * P].rearrange("p (u j) -> p j u", u=2),
                 )
             return h
 
-        def quantise(c, h):
-            codes = keep.tile([P, HALF], U32, name="h_codes%d" % c, align_bytes=64)
-            plane = keep.tile([P, HALF], U8, name="h_plane%d" % c, align_bytes=64)
+        def quantise(h, name, tag):
+            width = h.shape[1] // 4
+            codes = word_tile(name, tag, width)
+            plane = keep.tile([P, width], U8, name=name + "_plane", align_bytes=64)
             nc.vector.quantize_mx(out=codes[:].bitcast(FP8X4), scales=plane[:], in_=h[:])
             return codes, plane
 
         def product(m, hq, acc):
             codes, plane = hq
             nc.tensor.matmul_mx(
-                acc[:],
+                acc,
                 lhsT=wd[:, m * P : (m + 1) * P].bitcast(FP8X4),
                 lhsT_scale=w_sc[:, 4 * R + m * P : 4 * R + (m + 1) * P],
                 rhs=codes[:].bitcast(FP8X4),
@@ -158,8 +163,8 @@ def tile_list_msg_relu_bias_kernel(
                 stop=True,
             )
 
-        def add_bias(m, c, acc, y):
-            nc.scalar.activation(y[:, c * HALF : (c + 1) * HALF], acc[:], ACT.Identity, bias=bias[:, m : m + 1])
+        def add_bias(m, y, acc):
+            nc.scalar.activation(y, acc, ACT.Identity, bias=bias[:, m : m + 1])
 
         def place(page, y, lo, hi):
             nc.vector.tensor_tensor(page[:].indirect(entries(dst_list, lo, hi)), y[:, lo:hi], weight[:, lo:hi], MULT)
@@ -168,73 +173,77 @@ def tile_list_msg_relu_bias_kernel(
             nc.sync.dma_start(out[m * P : (m + 1) * P, :], page[:])
 
         quarter = HALF // 2
-        s0 = word_tile("s0_0", "s0", HALF)
+        s0 = word_tile("s0_x", "s0_x", HALF)
         gather_words(s0[:], tab0, src_list, 0, HALF)
-        nc.vector.tensor_copy(src_sc[:], tab_sc[:].indirect(src_list[:]))
-        nc.sync.dma_start(src_sc1[0 : P - 4, :].bitcast(I32), src_sc[4:P, :].bitcast(I32))
-        nc.sync.dma_start(wd[:].bitcast(I32), words(wd_words[0]))
-        load_planes(wd_scales, 4 * R)
-        nc.sync.dma_start(weight[:], wgo)
-        with nc.allow_non_contiguous_dma(reason="one bias value a partition"):
-            nc.sync.dma_start(bias[:], b.rearrange("(m p) -> p m", p=P))
-        dst_sc = gather_dst_scales(0, "dst_sc")
-        d0 = word_tile("d0_0", "d0", HALF)
+        nc.vector.tensor_copy(dst_sc[:], tab_sc[:].indirect(dst_list[:]))
+        d0 = word_tile("d0_x", "d0_x", HALF)
         gather_words(d0[:], tab0, dst_list, 0, HALF)
         d1, s1 = [], []
         for g in range(2):
-            d1.append(word_tile("d1_%d" % g, "hold_s0" if g == 0 else "d1b", quarter))
+            d1.append(word_tile("d1_%d" % g, "d1_%d" % g, quarter))
             gather_words(d1[g][:], tab1, dst_list, g * quarter, (g + 1) * quarter)
             s1.append(word_tile("s1_%d" % g, "s1_%d" % g, quarter))
             gather_words(s1[g][:], tab1, src_list, g * quarter, (g + 1) * quarter)
         for i, picked in ((0, s0), (1, d0)):
             for jt in range(TILES):
-                mx_pass(0, jt, i, cols(picked, jt), dst_sc)
-        for jt in range(TILES):
-            mx_pass(0, jt, 2, cols(d1[jt // 2], jt % 2), dst_sc)
-            mx_pass(0, jt, 3, cols(s1[jt // 2], jt % 2), dst_sc)
-
-        s0 = word_tile("s0_1", "hold_s0", HALF)
-        gather_words(s0[:], tab0, src_list, HALF, J)
-        d0 = word_tile("d0_1", "d0", HALF)
-        gather_words(d0[:], tab0, dst_list, HALF, J)
-        h0 = hidden(0, bank[4:8])
-        dst_sc = gather_dst_scales(1, "dst_sc")
-        hq0 = quantise(0, h0)
-        late = word_tile("late", "h0", J)
+                mx_pass(jt, i, cols(picked, jt))
+        h = []
         for g in range(2):
-            gather_words(late[:, 2 * g * quarter : (2 * g + 1) * quarter], tab1, dst_list, HALF + g * quarter, HALF + (g + 1) * quarter)
-            gather_words(late[:, (2 * g + 1) * quarter : (2 * g + 2) * quarter], tab1, src_list, HALF + g * quarter, HALF + (g + 1) * quarter)
-        y0 = keep.tile([P, J], F32, name="y0")
-        product(0, hq0, bank[0])
-        add_bias(0, 0, bank[0], y0)
-        product(1, hq0, bank[1])
-        place(page_a, y0, 0, HALF)
+            for jt in range(2):
+                mx_pass(2 * g + jt, 2, cols(d1[g], jt))
+                mx_pass(2 * g + jt, 3, cols(s1[g], jt))
+            h.append(hidden("h_%d" % g, (2 * g, 2 * g + 1)))
+
+        page_c = keep.tile([P, T], F32, name="page_c", tag="s0_x", align_bytes=64)
+        nc.gpsimd.memset(page_c[:], 0.0)
+
+        s0 = word_tile("s0_y", "d1_0", HALF)
+        gather_words(s0[:], tab0, src_list, HALF, J)
+        d0 = word_tile("d0_y", "s1_0", HALF)
+        gather_words(d0[:], tab0, dst_list, HALF, J)
+        late = []
+        for g, tag in enumerate(("relu1", "h_0")):
+            if g == 1:
+                hq_a = quantise(h[0], "hq_a", "hq_a")
+            lo = HALF + g * quarter
+            late.append(word_tile("late%d" % g, tag, HALF))
+            gather_words(late[g][:, 0:quarter], tab1, dst_list, lo, lo + quarter)
+            gather_words(late[g][:, quarter:HALF], tab1, src_list, lo, lo + quarter)
+        hq_b = quantise(h[1], "hq_b", "hq_b")
+
+        y0 = keep.tile([P, J], F32, name="y0", tag="relu3", align_bytes=64)
+        y1 = keep.tile([P, J], F32, name="y1")
+        y3 = keep.tile([P, J], F32, name="y3")
+        product(0, hq_a, bank[0][:, 0:quarter])
+        add_bias(0, y0[:, 0:quarter], bank[0][:, 0:quarter])
+        place(page_a, y0, 0, quarter)
+        for m in range(1, 4):
+            product(m, hq_a, bank[m][:, 0:quarter])
+        for m in (1, 0, 2, 3):
+            product(m, hq_b, bank[m][:, quarter:HALF])
+        add_bias(1, y1[:, 0:HALF], bank[1][:])
+        place(page_b, y1, 0, HALF)
+        add_bias(0, y0[:, quarter:HALF], bank[0][:, quarter:HALF])
+        place(page_a, y0, quarter, HALF)
+        add_bias(3, y3[:, 0:HALF], bank[3][:])
 
         for i, picked in ((0, s0), (1, d0)):
             for jt in range(TILES):
-                mx_pass(1, jt, i, cols(picked, jt), dst_sc)
+                mx_pass(TILES + jt, i, cols(picked, jt))
         for jt in range(TILES):
-            mx_pass(1, jt, 2, cols(late, 4 * (jt // 2) + jt % 2), dst_sc)
-            mx_pass(1, jt, 3, cols(late, 4 * (jt // 2) + 2 + jt % 2), dst_sc)
-        hq1 = quantise(1, hidden(1, bank[4:8]))
+            mx_pass(TILES + jt, 2, cols(late[jt // 2], jt % 2))
+            mx_pass(TILES + jt, 3, cols(late[jt // 2], 2 + jt % 2))
+        hq_c = quantise(hidden("h_c", (4, 5, 6, 7)), "hq_c", "hq_c")
 
-        y1 = keep.tile([P, J], F32, name="y1", tag="relu3", align_bytes=64)
-        add_bias(1, 0, bank[1], y1)
-        cover = 3 * P
-        place(page_b, y1, 0, cover)
-        product(0, hq1, bank[2])
-        add_bias(0, 1, bank[2], y0)
-        place(page_a, y0, HALF, J)
-        store(0, page_a)
-        product(1, hq1, bank[3])
-        add_bias(1, 1, bank[3], y1)
-        place(page_b, y1, cover, J)
-        store(1, page_b)
-        for m, page in ((2, page_a), (3, page_b)):
-            y = keep.tile([P, J], F32, name="y%d" % m)
-            product(m, hq0, bank[m + 4])
-            add_bias(m, 0, bank[m + 4], y)
-            product(m, hq1, bank[m + 2])
-            add_bias(m, 1, bank[m + 2], y)
-            place(page, y, 0, J)
+        y2 = keep.tile([P, J], F32, name="y2", tag="relu7", align_bytes=64)
+        add_bias(2, y2[:, 0:HALF], bank[2][:])
+        place(page_c, y2, 0, HALF)
+        for m, y, page, acc in ((0, y0, page_a, 0), (1, y1, page_b, 1), (2, y2, page_c, 3)):
+            product(m, hq_c, bank[acc][:])
+            add_bias(m, y[:, HALF:J], bank[acc][:])
+            place(page, y, HALF, J)
             store(m, page)
+        product(3, hq_c, bank[4][:])
+        add_bias(3, y3[:, HALF:J], bank[4][:])
+        place(page_a, y3, 0, J)
+        store(3, page_a)

@@ -46,6 +46,7 @@ def tile_list_msg_relu_bias_kernel(
         weight = keep.tile([P, J], F32, name="weight")
         bias = keep.tile([P, N // P], F32, name="bias")
         ident = keep.tile([P, P], F32, name="ident")
+        bias_rows = keep.tile([P, P], F32, name="bias_rows")
         page_a = keep.tile([P, T], F32, name="page_a")
         page_b = keep.tile([P, T], F32, name="page_b")
         bank = [psum.tile([P, R], F32, name="bank%d" % i) for i in range(8)]
@@ -53,6 +54,7 @@ def tile_list_msg_relu_bias_kernel(
         nc.vector.memset(tab_sc[:].bitcast(I32), 0)
         nc.vector.memset(w_sc[:].bitcast(I32), 0)
         nc.vector.memset(src_sc1[:].bitcast(I32), 0)
+        nc.vector.memset(bias_rows[:].bitcast(I32), 0)
         nc.vector.memset(page_a[:].bitcast(I32), 0)
         nc.vector.memset(page_b[:].bitcast(I32), 0)
         make_identity(nc, ident[:])
@@ -89,8 +91,7 @@ def tile_list_msg_relu_bias_kernel(
         nc.sync.dma_start(src_sc1[0 : P - 4, :].bitcast(I32), src_sc[4:P, :].bitcast(I32))
         nc.sync.dma_start(wd[:].bitcast(I32), words(wd_words[0]))
         load_planes(wd_scales, 4 * R)
-        with nc.allow_non_contiguous_dma(reason="one bias value a partition"):
-            nc.sync.dma_start(bias[:], b.rearrange("(m p) -> p m", p=P))
+        nc.sync.dma_start(bias_rows[0 : N // P, :], b.rearrange("(m p) -> m p", p=P))
         nc.sync.dma_start(weight[:], wgo)
 
         def entries(lst, lo, hi):
@@ -193,6 +194,8 @@ def tile_list_msg_relu_bias_kernel(
                 mx_pass(2 * g + jt, 2, cols(d1[g], jt))
                 mx_pass(2 * g + jt, 3, cols(s1[g], jt))
             h.append(hidden("h_%d" % g, (2 * g, 2 * g + 1)))
+        nc.tensor.transpose(bank[3][:, 0:P], bias_rows[:], ident[:])
+        nc.scalar.copy(bias[:], bank[3][:, 0 : N // P])
 
         page_c = keep.tile([P, T], F32, name="page_c", tag="s0_x", align_bytes=64)
         nc.gpsimd.memset(page_c[:], 0.0)

@@ -29,6 +29,7 @@ def tile_list_msg_relu_bias_kernel(
     nc = tc.nc
     with ExitStack() as ctx:
         keep = ctx.enter_context(tc.tile_pool(name="keep", bufs=1))
+        shared = ctx.enter_context(tc.tile_pool(name="shared", bufs=1))
         psum = ctx.enter_context(tc.psum_pool(name="psum", bufs=1))
 
         src_list = keep.tile([P, J // 16], U16, name="src_list")
@@ -46,17 +47,13 @@ def tile_list_msg_relu_bias_kernel(
         weight = keep.tile([P, J], F32, name="weight")
         bias = keep.tile([P, N // P], F32, name="bias")
         ident = keep.tile([P, P], F32, name="ident")
-        bias_rows = keep.tile([P, P], F32, name="bias_rows")
         page_a = keep.tile([P, T], F32, name="page_a")
-        page_b = keep.tile([P, T], F32, name="page_b")
         bank = [psum.tile([P, R], F32, name="bank%d" % i) for i in range(8)]
 
         nc.vector.memset(tab_sc[:].bitcast(I32), 0)
         nc.vector.memset(w_sc[:].bitcast(I32), 0)
         nc.vector.memset(src_sc1[:].bitcast(I32), 0)
-        nc.vector.memset(bias_rows[:].bitcast(I32), 0)
         nc.vector.memset(page_a[:].bitcast(I32), 0)
-        nc.vector.memset(page_b[:].bitcast(I32), 0)
         make_identity(nc, ident[:])
 
         def words(ap):
@@ -91,7 +88,8 @@ def tile_list_msg_relu_bias_kernel(
         nc.sync.dma_start(src_sc1[0 : P - 4, :].bitcast(I32), src_sc[4:P, :].bitcast(I32))
         nc.sync.dma_start(wd[:].bitcast(I32), words(wd_words[0]))
         load_planes(wd_scales, 4 * R)
-        nc.sync.dma_start(bias_rows[0 : N // P, :], b.rearrange("(m p) -> m p", p=P))
+        with nc.allow_non_contiguous_dma(reason="one bias value a partition"):
+            nc.sync.dma_start(bias[:], b.rearrange("(m p) -> p m", p=P))
         nc.sync.dma_start(weight[:], wgo)
 
         def entries(lst, lo, hi):
@@ -123,9 +121,8 @@ def tile_list_msg_relu_bias_kernel(
         def cols(t, jt):
             return t[:, jt * P : (jt + 1) * P]
 
-        def hidden(name, tiles):
+        def hidden(h, tiles):
             relu = [keep.tile([P, R], BF16, name="relu%d" % jt, tag="relu%d" % jt, align_bytes=64) for jt in tiles]
-            h = keep.tile([P, 4 * P * len(tiles)], BF16, name=name, tag=name, align_bytes=64)
             turn = [bank[TILES + jt % TILES] for jt in tiles]
             for i, jt in enumerate(tiles):
                 nc.scalar.activation(
@@ -143,7 +140,6 @@ def tile_list_msg_relu_bias_kernel(
                     h_pairs[:, 2 * P * i : 2 * P * (i + 1)].rearrange("p (j u) -> p j u", u=2),
                     turn[i][:, 0 : 2 * P].rearrange("p (u j) -> p j u", u=2),
                 )
-            return h
 
         def quantise(h, name, tag):
             width = h.shape[1] // 4
@@ -188,31 +184,31 @@ def tile_list_msg_relu_bias_kernel(
         for i, picked in ((0, s0), (1, d0)):
             for jt in range(TILES):
                 mx_pass(jt, i, cols(picked, jt))
-        h = []
+        h = [
+            keep.tile([P, 4 * quarter], BF16, name="h_0", tag="h_0", align_bytes=64),
+            shared.tile([P, 4 * quarter], BF16, name="h_1", offset=4 * T - 4 * quarter, align_bytes=64),
+        ]
         for g in range(2):
             for jt in range(2):
                 mx_pass(2 * g + jt, 2, cols(d1[g], jt))
                 mx_pass(2 * g + jt, 3, cols(s1[g], jt))
-            h.append(hidden("h_%d" % g, (2 * g, 2 * g + 1)))
-        nc.tensor.transpose(bank[3][:, 0:P], bias_rows[:], ident[:])
-        nc.scalar.copy(bias[:], bank[3][:, 0 : N // P])
+            hidden(h[g], (2 * g, 2 * g + 1))
 
-        page_c = keep.tile([P, T], F32, name="page_c", tag="s0_x", align_bytes=64)
-        nc.gpsimd.memset(page_c[:], 0.0)
 
         s0 = word_tile("s0_y", "d1_0", HALF)
         gather_words(s0[:], tab0, src_list, HALF, J)
         d0 = word_tile("d0_y", "s1_0", HALF)
         gather_words(d0[:], tab0, dst_list, HALF, J)
-        late = []
-        for g, tag in enumerate(("relu1", "h_0")):
-            if g == 1:
-                hq_a = quantise(h[0], "hq_a", "hq_a")
-            lo = HALF + g * quarter
-            late.append(word_tile("late%d" % g, tag, HALF))
-            gather_words(late[g][:, 0:quarter], tab1, dst_list, lo, lo + quarter)
-            gather_words(late[g][:, quarter:HALF], tab1, src_list, lo, lo + quarter)
+        d1 = word_tile("d1_y", "d0_x", HALF)
+        gather_words(d1[:], tab1, dst_list, HALF, J)
+        hq_a = quantise(h[0], "hq_a", "hq_a")
+        s1 = word_tile("s1_y", "h_0", HALF)
+        gather_words(s1[:], tab1, src_list, HALF, J)
         hq_b = quantise(h[1], "hq_b", "hq_b")
+        page_b = shared.tile([P, T], F32, name="page_b", offset=0)
+        nc.gpsimd.memset(page_b[:], 0.0)
+        page_c = shared.tile([P, T], F32, name="page_c", offset=4 * T)
+        nc.gpsimd.memset(page_c[:], 0.0)
 
         y0 = keep.tile([P, J], F32, name="y0", tag="relu3", align_bytes=64)
         y1 = keep.tile([P, J], F32, name="y1")
@@ -222,21 +218,23 @@ def tile_list_msg_relu_bias_kernel(
         place(page_a, y0, 0, quarter)
         for m in range(1, 4):
             product(m, hq_a, bank[m][:, 0:quarter])
-        for m in (1, 0, 2, 3):
+        for m in range(4):
             product(m, hq_b, bank[m][:, quarter:HALF])
-        add_bias(1, y1[:, 0:HALF], bank[1][:])
-        place(page_b, y1, 0, HALF)
         add_bias(0, y0[:, quarter:HALF], bank[0][:, quarter:HALF])
         place(page_a, y0, quarter, HALF)
+        add_bias(1, y1[:, 0:HALF], bank[1][:])
+        place(page_b, y1, 0, HALF)
         add_bias(3, y3[:, 0:HALF], bank[3][:])
 
         for i, picked in ((0, s0), (1, d0)):
             for jt in range(TILES):
                 mx_pass(TILES + jt, i, cols(picked, jt))
         for jt in range(TILES):
-            mx_pass(TILES + jt, 2, cols(late[jt // 2], jt % 2))
-            mx_pass(TILES + jt, 3, cols(late[jt // 2], 2 + jt % 2))
-        hq_c = quantise(hidden("h_c", (4, 5, 6, 7)), "hq_c", "hq_c")
+            mx_pass(TILES + jt, 2, cols(d1, jt))
+            mx_pass(TILES + jt, 3, cols(s1, jt))
+        h_c = keep.tile([P, 4 * HALF], BF16, name="h_c", align_bytes=64)
+        hidden(h_c, (4, 5, 6, 7))
+        hq_c = quantise(h_c, "hq_c", "hq_c")
 
         y2 = keep.tile([P, J], F32, name="y2", tag="relu7", align_bytes=64)
         add_bias(2, y2[:, 0:HALF], bank[2][:])

@@ -29,14 +29,13 @@ def tile_list_msg_relu_bias_kernel(
     nc = tc.nc
     with ExitStack() as ctx:
         keep = ctx.enter_context(tc.tile_pool(name="keep", bufs=1))
-        shared = ctx.enter_context(tc.tile_pool(name="shared", bufs=1))
         psum = ctx.enter_context(tc.psum_pool(name="psum", bufs=1))
 
         src_list = keep.tile([P, J // 16], U16, name="src_list")
         dst_list = keep.tile([P, J // 16], U16, name="dst_list")
         tab0 = keep.tile([P, T], I32, name="tab0", align_bytes=64)
         tab1 = keep.tile([P, T], I32, name="tab1", align_bytes=64)
-        tab_sc = keep.tile([P, T], U8, name="tab_sc", align_bytes=64)
+        tab_sc = keep.tile([P, T], U8, name="tab_sc", tag="tab_sc", align_bytes=64)
         ws = keep.tile([P, 2 * 2 * R], U8, name="ws", align_bytes=64)
         wt = keep.tile([P, 2 * R], U32, name="wt", align_bytes=64)
         w_sc = keep.tile([P, 5 * R], U8, name="w_sc", align_bytes=64)
@@ -46,15 +45,15 @@ def tile_list_msg_relu_bias_kernel(
         wd = keep.tile([P, N], U32, name="wd", align_bytes=64)
         weight = keep.tile([P, J], F32, name="weight")
         bias = keep.tile([P, N // P], F32, name="bias")
-        ident = keep.tile([P, P], F32, name="ident")
         page_a = keep.tile([P, T], F32, name="page_a")
+        page_b = keep.tile([P, T], F32, name="page_b")
         bank = [psum.tile([P, R], F32, name="bank%d" % i) for i in range(8)]
 
         nc.vector.memset(tab_sc[:].bitcast(I32), 0)
         nc.vector.memset(w_sc[:].bitcast(I32), 0)
         nc.vector.memset(src_sc1[:].bitcast(I32), 0)
         nc.vector.memset(page_a[:].bitcast(I32), 0)
-        make_identity(nc, ident[:])
+        nc.vector.memset(page_b[:].bitcast(I32), 0)
 
         def words(ap):
             return ap.rearrange("p t i -> p (t i)").bitcast(I32)
@@ -173,6 +172,8 @@ def tile_list_msg_relu_bias_kernel(
         s0 = word_tile("s0_x", "s0_x", HALF)
         gather_words(s0[:], tab0, src_list, 0, HALF)
         nc.vector.tensor_copy(dst_sc[:], tab_sc[:].indirect(dst_list[:]))
+        ident = keep.tile([P, P], F32, name="ident", tag="tab_sc", align_bytes=64)
+        make_identity(nc, ident[:])
         d0 = word_tile("d0_x", "d0_x", HALF)
         gather_words(d0[:], tab0, dst_list, 0, HALF)
         d1, s1 = [], []
@@ -186,7 +187,7 @@ def tile_list_msg_relu_bias_kernel(
                 mx_pass(jt, i, cols(picked, jt))
         h = [
             keep.tile([P, 4 * quarter], BF16, name="h_0", tag="h_0", align_bytes=64),
-            shared.tile([P, 4 * quarter], BF16, name="h_1", offset=4 * T - 4 * quarter, align_bytes=64),
+            keep.tile([P, 4 * quarter], BF16, name="h_1", tag="h_1", align_bytes=64),
         ]
         for g in range(2):
             for jt in range(2):
@@ -205,9 +206,7 @@ def tile_list_msg_relu_bias_kernel(
         s1 = word_tile("s1_y", "h_0", HALF)
         gather_words(s1[:], tab1, src_list, HALF, J)
         hq_b = quantise(h[1], "hq_b", "hq_b")
-        page_b = shared.tile([P, T], F32, name="page_b", offset=0)
-        nc.gpsimd.memset(page_b[:], 0.0)
-        page_c = shared.tile([P, T], F32, name="page_c", offset=4 * T)
+        page_c = keep.tile([P, T], F32, name="page_c", tag="h_1", align_bytes=64)
         nc.gpsimd.memset(page_c[:], 0.0)
 
         y0 = keep.tile([P, J], F32, name="y0", tag="relu3", align_bytes=64)
@@ -218,12 +217,12 @@ def tile_list_msg_relu_bias_kernel(
         place(page_a, y0, 0, quarter)
         for m in range(1, 4):
             product(m, hq_a, bank[m][:, 0:quarter])
-        for m in range(4):
+        for m in (1, 0, 2, 3):
             product(m, hq_b, bank[m][:, quarter:HALF])
-        add_bias(0, y0[:, quarter:HALF], bank[0][:, quarter:HALF])
-        place(page_a, y0, quarter, HALF)
         add_bias(1, y1[:, 0:HALF], bank[1][:])
         place(page_b, y1, 0, HALF)
+        add_bias(0, y0[:, quarter:HALF], bank[0][:, quarter:HALF])
+        place(page_a, y0, quarter, HALF)
         add_bias(3, y3[:, 0:HALF], bank[3][:])
 
         for i, picked in ((0, s0), (1, d0)):

@@ -67,9 +67,7 @@ def tile_list_msg_relu_bias_kernel(
                 )
 
         nc.sync.dma_start(src_list[:], offs)
-        nc.sync.dma_start(
-            ws[:].bitcast(I32).rearrange("p (a w) -> p a w", a=2), ws_words.bitcast(I32).rearrange("a p w -> p a w")
-        )
+        nc.sync.dma_start(ws[:, 0 : 2 * R].bitcast(I32), ws_words[0].bitcast(I32))
         for q in range(4):
             nc.sync.dma_start(
                 tab_sc[32 * q : 32 * q + 8, :].bitcast(I32), tab_scales[:, 4 * q : 4 * q + 4, :].bitcast(I32)
@@ -83,6 +81,7 @@ def tile_list_msg_relu_bias_kernel(
         )
         nc.sync.dma_start(tab1[:], words(tab_words[1]))
         load_planes(wt_scales, 2 * R)
+        nc.sync.dma_start(ws[:, 2 * R : 4 * R].bitcast(I32), ws_words[1].bitcast(I32))
         nc.vector.tensor_copy(src_sc[:], tab_sc[:].indirect(src_list[:]))
         nc.sync.dma_start(src_sc1[0 : P - 4, :].bitcast(I32), src_sc[4:P, :].bitcast(I32))
         nc.sync.dma_start(wd[:].bitcast(I32), words(wd_words[0]))

@@ -38,10 +38,8 @@ def tile_list_msg_relu_bias_kernel(
         tab_sc = keep.tile([P, T], U8, name="tab_sc", tag="tab_sc", align_bytes=64)
         ws = keep.tile([P, 2 * 2 * R], U8, name="ws", align_bytes=64)
         wt = keep.tile([P, 2 * R], U32, name="wt", align_bytes=64)
-        w_sc = keep.tile([P, 5 * R], U8, name="w_sc", align_bytes=64)
-        src_sc = keep.tile([P, J], U8, name="src_sc", align_bytes=64)
-        dst_sc = keep.tile([P, J], U8, name="dst_sc", align_bytes=64)
-        src_sc1 = keep.tile([P, J], U8, name="src_sc1", align_bytes=64)
+        w_sc = keep.tile([P, 3 * R], U8, name="w_sc", align_bytes=64)
+        sc0 = keep.tile([P, 2 * J], U8, name="sc0", align_bytes=64)
         wd = keep.tile([P, N], U32, name="wd", align_bytes=64)
         weight = keep.tile([P, J], F32, name="weight")
         bias = keep.tile([P, N // P], F32, name="bias")
@@ -51,7 +49,6 @@ def tile_list_msg_relu_bias_kernel(
 
         nc.vector.memset(tab_sc[:].bitcast(I32), 0)
         nc.vector.memset(w_sc[:].bitcast(I32), 0)
-        nc.vector.memset(src_sc1[:].bitcast(I32), 0)
         nc.vector.memset(page_a[:].bitcast(I32), 0)
         nc.vector.memset(page_b[:].bitcast(I32), 0)
 
@@ -67,25 +64,26 @@ def tile_list_msg_relu_bias_kernel(
                 )
 
         nc.sync.dma_start(src_list[:], offs)
+        nc.sync.dma_start(dst_list[:], offs2)
+        by_row = tab_scales.bitcast(I32).rearrange("a (q r) w -> r q a w", r=4)
+        for r in range(4):
+            nc.sync.dma_start(tab_sc[r:P:16, :].bitcast(I32), by_row[r])
+        nc.sync.dma_start(tab0[:], words(tab_words[0]))
         nc.sync.dma_start(ws[:, 0 : 2 * R].bitcast(I32), ws_words[0].bitcast(I32))
+        load_planes(ws_scales, 0)
+        nc.sync.dma_start(wt[:, 0:R].bitcast(I32), words(wt_words[0]))
+        nc.sync.dma_start(tab1[:], words(tab_words[1]))
         for q in range(4):
             nc.sync.dma_start(
-                tab_sc[32 * q : 32 * q + 8, :].bitcast(I32), tab_scales[:, 4 * q : 4 * q + 4, :].bitcast(I32)
+                w_sc[32 * q : 32 * q + 8, 2 * R : 3 * R].bitcast(I32), wt_scales[:, 4 * q : 4 * q + 4, :].bitcast(I32)
             )
-        nc.sync.dma_start(tab0[:], words(tab_words[0]))
-        nc.sync.dma_start(dst_list[:], offs2)
-        load_planes(ws_scales, 0)
-        nc.sync.dma_start(
-            wt[:].bitcast(I32).rearrange("p (a w) -> p a w", a=2),
-            wt_words.rearrange("a p r i -> a p (r i)").bitcast(I32).rearrange("a p w -> p a w"),
-        )
-        nc.sync.dma_start(tab1[:], words(tab_words[1]))
-        load_planes(wt_scales, 2 * R)
+        nc.sync.dma_start(wt[:, R : 2 * R].bitcast(I32), words(wt_words[1]))
         nc.sync.dma_start(ws[:, 2 * R : 4 * R].bitcast(I32), ws_words[1].bitcast(I32))
-        nc.vector.tensor_copy(src_sc[:], tab_sc[:].indirect(src_list[:]))
-        nc.sync.dma_start(src_sc1[0 : P - 4, :].bitcast(I32), src_sc[4:P, :].bitcast(I32))
+        nc.vector.tensor_copy(sc0[:, 0:J], tab_sc[:].indirect(src_list[:]))
+        nc.vector.tensor_copy(sc0[:, J : 2 * J], tab_sc[:].indirect(dst_list[:]))
+        sc1 = keep.tile([P, 2 * J], U8, name="sc1", tag="tab_sc", align_bytes=64)
+        nc.sync.dma_start(sc1[0 : P - 16, :].bitcast(I32), sc0[16:P, :].bitcast(I32))
         nc.sync.dma_start(wd[:].bitcast(I32), words(wd_words[0]))
-        load_planes(wd_scales, 4 * R)
         with nc.allow_non_contiguous_dma(reason="one bias value a partition"):
             nc.sync.dma_start(bias[:], b.rearrange("(m p) -> p m", p=P))
         nc.sync.dma_start(weight[:], wgo)
@@ -99,21 +97,23 @@ def tile_list_msg_relu_bias_kernel(
         def word_tile(name, tag, width):
             return keep.tile([P, width], U32, name=name, tag=tag, align_bytes=64)
 
-        def mx_pass(jt, i, picked):
-            plane, row, w, w_plane = (
-                (src_sc, 0, ws[:, 0 : 2 * R].bitcast(FP4X4), w_sc[:, 0:R]),
-                (dst_sc, 0, wt[:, 0:R].bitcast(FP8X4), w_sc[:, 2 * R : 3 * R]),
-                (dst_sc, 4, wt[:, R : 2 * R].bitcast(FP8X4), w_sc[:, 3 * R : 4 * R]),
-                (src_sc1, 0, ws[:, 2 * R : 4 * R].bitcast(FP4X4), w_sc[:, R : 2 * R]),
+        def mx_pass(jt, i, picked, first=0, last=3):
+            src = slice(jt * P, (jt + 1) * P)
+            dst = slice(J + jt * P, J + (jt + 1) * P)
+            plane, w, w_plane = (
+                (sc0[:, src], ws[:, 0 : 2 * R].bitcast(FP4X4), w_sc[:, 0:R]),
+                (sc0[:, dst], wt[:, 0:R].bitcast(FP8X4), w_sc[:, 2 * R : 3 * R]),
+                (sc1[:, dst], wt[:, R : 2 * R].bitcast(FP8X4), w_sc[4:P, 2 * R : 3 * R]),
+                (sc1[:, src], ws[:, 2 * R : 4 * R].bitcast(FP4X4), w_sc[:, R : 2 * R]),
             )[i]
             nc.tensor.matmul_mx(
                 bank[jt][:],
                 lhsT=picked.bitcast(FP8X4),
-                lhsT_scale=plane[row:P, jt * P : (jt + 1) * P],
+                lhsT_scale=plane,
                 rhs=w,
                 rhs_scale=w_plane,
-                start=(i == 0),
-                stop=(i == 3),
+                start=(i == first),
+                stop=(i == last),
             )
 
         def cols(t, jt):
@@ -151,7 +151,7 @@ def tile_list_msg_relu_bias_kernel(
             nc.tensor.matmul_mx(
                 acc,
                 lhsT=wd[:, m * P : (m + 1) * P].bitcast(FP8X4),
-                lhsT_scale=w_sc[:, 4 * R + m * P : 4 * R + (m + 1) * P],
+                lhsT_scale=wd_sc[:, m * P : (m + 1) * P],
                 rhs=codes[:].bitcast(FP8X4),
                 rhs_scale=plane[:],
                 start=True,
@@ -168,22 +168,26 @@ def tile_list_msg_relu_bias_kernel(
             nc.sync.dma_start(out[m * P : (m + 1) * P, :], page[:])
 
         quarter = HALF // 2
-        s0 = word_tile("s0_x", "s0_x", HALF)
-        gather_words(s0[:], tab0, src_list, 0, HALF)
-        nc.vector.tensor_copy(dst_sc[:], tab_sc[:].indirect(dst_list[:]))
-        ident = keep.tile([P, P], F32, name="ident", tag="tab_sc", align_bytes=64)
-        make_identity(nc, ident[:])
-        d0 = word_tile("d0_x", "d0_x", HALF)
-        gather_words(d0[:], tab0, dst_list, 0, HALF)
-        d1, s1 = [], []
+        s0, d0, d1, s1 = [], [], [], []
+        for g in range(2):
+            s0.append(word_tile("s0_%d" % g, "s0_%d" % g, quarter))
+            gather_words(s0[g][:], tab0, src_list, g * quarter, (g + 1) * quarter)
+            d0.append(word_tile("d0_%d" % g, "d0_%d" % g, quarter))
+            gather_words(d0[g][:], tab0, dst_list, g * quarter, (g + 1) * quarter)
         for g in range(2):
             d1.append(word_tile("d1_%d" % g, "d1_%d" % g, quarter))
             gather_words(d1[g][:], tab1, dst_list, g * quarter, (g + 1) * quarter)
             s1.append(word_tile("s1_%d" % g, "s1_%d" % g, quarter))
             gather_words(s1[g][:], tab1, src_list, g * quarter, (g + 1) * quarter)
-        for i, picked in ((0, s0), (1, d0)):
-            for jt in range(TILES):
-                mx_pass(jt, i, cols(picked, jt))
+        for g in range(2):
+            for i, picked in ((0, s0), (1, d0)):
+                for jt in range(2):
+                    mx_pass(2 * g + jt, i, cols(picked[g], jt))
+        ident = keep.tile([P, P], F32, name="ident", tag="s0_0", align_bytes=64)
+        make_identity(nc, ident[:])
+        wd_sc = keep.tile([P, N], U8, name="wd_sc", tag="d0_0", align_bytes=64)
+        for q in range(4):
+            nc.sync.dma_start(wd_sc[32 * q : 32 * q + 4, :].bitcast(I32), wd_scales[0, 4 * q : 4 * q + 4, :].bitcast(I32))
         h = [
             keep.tile([P, 4 * quarter], BF16, name="h_0", tag="h_0", align_bytes=64),
             keep.tile([P, 4 * quarter], BF16, name="h_1", tag="h_1", align_bytes=64),
@@ -195,15 +199,15 @@ def tile_list_msg_relu_bias_kernel(
             hidden(h[g], (2 * g, 2 * g + 1))
 
 
+        d1 = word_tile("d1_y", "d1_y", HALF)
+        gather_words(d1[:], tab1, dst_list, HALF, J)
+        s1 = word_tile("s1_y", "s1_y", HALF)
+        gather_words(s1[:], tab1, src_list, HALF, J)
         s0 = word_tile("s0_y", "d1_0", HALF)
         gather_words(s0[:], tab0, src_list, HALF, J)
-        d0 = word_tile("d0_y", "s1_0", HALF)
-        gather_words(d0[:], tab0, dst_list, HALF, J)
-        d1 = word_tile("d1_y", "d0_x", HALF)
-        gather_words(d1[:], tab1, dst_list, HALF, J)
         hq_a = quantise(h[0], "hq_a", "hq_a")
-        s1 = word_tile("s1_y", "h_0", HALF)
-        gather_words(s1[:], tab1, src_list, HALF, J)
+        d0 = word_tile("d0_y", "h_0", HALF)
+        gather_words(d0[:], tab0, dst_list, HALF, J)
         hq_b = quantise(h[1], "hq_b", "hq_b")
         page_c = keep.tile([P, T], F32, name="page_c", tag="h_1", align_bytes=64)
         nc.gpsimd.memset(page_c[:], 0.0)
@@ -224,12 +228,12 @@ def tile_list_msg_relu_bias_kernel(
         place(page_a, y0, quarter, HALF)
         add_bias(3, y3[:, 0:HALF], bank[3][:])
 
-        for i, picked in ((0, s0), (1, d0)):
+        for i, picked in ((2, d1), (3, s1)):
             for jt in range(TILES):
-                mx_pass(TILES + jt, i, cols(picked, jt))
+                mx_pass(TILES + jt, i, cols(picked, jt), 2, 1)
         for jt in range(TILES):
-            mx_pass(TILES + jt, 2, cols(d1, jt))
-            mx_pass(TILES + jt, 3, cols(s1, jt))
+            mx_pass(TILES + jt, 0, cols(s0, jt), 2, 1)
+            mx_pass(TILES + jt, 1, cols(d0, jt), 2, 1)
         h_c = keep.tile([P, 4 * HALF], BF16, name="h_c", align_bytes=64)
         hidden(h_c, (4, 5, 6, 7))
         hq_c = quantise(h_c, "hq_c", "hq_c")

@@ -211,42 +211,43 @@ def tile_list_msg_relu_bias_kernel(
         hq_b = quantise(h[1], "hq_b", "hq_b")
         page_c = keep.tile([P, T], F32, name="page_c", tag="h_1", align_bytes=64)
         nc.gpsimd.memset(page_c[:], 0.0)
+        pages = (page_a, page_b, page_c)
+        y = [keep.tile([P, J], F32, name="y%d" % m) for m in range(1, 4)]
+        y.insert(0, keep.tile([P, J], F32, name="y0", tag="relu3", align_bytes=64))
 
-        y0 = keep.tile([P, J], F32, name="y0", tag="relu3", align_bytes=64)
-        y1 = keep.tile([P, J], F32, name="y1")
-        y3 = keep.tile([P, J], F32, name="y3")
-        product(0, hq_a, bank[0][:, 0:quarter])
-        add_bias(0, y0[:, 0:quarter], bank[0][:, 0:quarter])
-        place(page_a, y0, 0, quarter)
-        for m in range(1, 4):
-            product(m, hq_a, bank[m][:, 0:quarter])
-        for m in (1, 0, 2, 3):
-            product(m, hq_b, bank[m][:, quarter:HALF])
-        add_bias(1, y1[:, 0:HALF], bank[1][:])
-        place(page_b, y1, 0, HALF)
-        add_bias(0, y0[:, quarter:HALF], bank[0][:, quarter:HALF])
-        place(page_a, y0, quarter, HALF)
-        add_bias(3, y3[:, 0:HALF], bank[3][:])
+        def last_part(tiles, passes):
+            for jt in tiles:
+                for i in passes:
+                    mx_pass(TILES + jt, i, cols((s0, d0, d1, s1)[i], jt), 2, 1)
 
-        for i, picked in ((2, d1), (3, s1)):
-            for jt in range(TILES):
-                mx_pass(TILES + jt, i, cols(picked, jt), 2, 1)
-        for jt in range(TILES):
-            mx_pass(TILES + jt, 0, cols(s0, jt), 2, 1)
-            mx_pass(TILES + jt, 1, cols(d0, jt), 2, 1)
+        def message(m, hq, lo, hi, acc):
+            product(m, hq, acc)
+            add_bias(m, y[m][:, lo:hi], acc)
+
+        last_part((0, 1), (2, 3))
+        for m in range(2):
+            message(m, hq_a, 0, quarter, bank[m][:, 0:quarter])
+            place(pages[m], y[m], 0, quarter)
+        last_part((0, 1), (0,))
+        last_part((2,), (2, 3, 0))
+        last_part((0, 1, 2), (1,))
+        for m in range(2):
+            message(m, hq_b, quarter, HALF, bank[m][:, quarter:HALF])
+            place(pages[m], y[m], quarter, HALF)
+        last_part((3,), (2, 3, 0, 1))
         h_c = keep.tile([P, 4 * HALF], BF16, name="h_c", align_bytes=64)
         hidden(h_c, (4, 5, 6, 7))
         hq_c = quantise(h_c, "hq_c", "hq_c")
 
-        y2 = keep.tile([P, J], F32, name="y2", tag="relu7", align_bytes=64)
-        add_bias(2, y2[:, 0:HALF], bank[2][:])
-        place(page_c, y2, 0, HALF)
-        for m, y, page, acc in ((0, y0, page_a, 0), (1, y1, page_b, 1), (2, y2, page_c, 3)):
-            product(m, hq_c, bank[acc][:])
-            add_bias(m, y[:, HALF:J], bank[acc][:])
-            place(page, y, HALF, J)
-            store(m, page)
-        product(3, hq_c, bank[4][:])
-        add_bias(3, y3[:, HALF:J], bank[4][:])
-        place(page_a, y3, 0, J)
+        for m in (2, 3):
+            product(m, hq_a, bank[m + 2][:, 0:quarter])
+            product(m, hq_b, bank[m + 2][:, quarter:HALF])
+            add_bias(m, y[m][:, 0:HALF], bank[m + 2][:])
+        place(page_c, y[2], 0, HALF)
+        for m in range(3):
+            message(m, hq_c, HALF, J, bank[m][:])
+            place(pages[m], y[m], HALF, J)
+            store(m, pages[m])
+        message(3, hq_c, HALF, J, bank[3][:])
+        place(page_a, y[3], 0, J)
         store(3, page_a)

@@ -48,37 +48,38 @@ def tile_list_msg_relu_bias_kernel(
         bank = [psum.tile([P, R], F32, name="bank%d" % i) for i in range(8)]
 
         nc.vector.memset(tab_sc[:].bitcast(I32), 0)
-        nc.vector.memset(w_sc[:].bitcast(I32), 0)
         nc.vector.memset(page_a[:].bitcast(I32), 0)
         nc.vector.memset(page_b[:].bitcast(I32), 0)
 
         def words(ap):
             return ap.rearrange("p t i -> p (t i)").bitcast(I32)
 
-        def load_planes(scales, col):
-            passes = scales.shape[0]
-            for q in range(4):
-                nc.sync.dma_start(
-                    w_sc[32 * q : 32 * q + 4, col : col + passes * R].bitcast(I32).rearrange("p (a w) -> p a w", a=passes),
-                    scales[:, 4 * q : 4 * q + 4, :].bitcast(I32).rearrange("a r w -> r a w"),
-                )
+        def load_ws_rows(q):
+            nc.sync.dma_start(
+                w_sc[32 * q : 32 * q + 4, 0 : 2 * R].bitcast(I32).rearrange("p (a w) -> p a w", a=2),
+                ws_scales[:, 4 * q : 4 * q + 4, :].bitcast(I32).rearrange("a r w -> r a w"),
+            )
 
         nc.sync.dma_start(src_list[:], offs)
         nc.sync.dma_start(dst_list[:], offs2)
         by_row = tab_scales.bitcast(I32).rearrange("a (q r) w -> r q a w", r=4)
         for r in range(4):
             nc.sync.dma_start(tab_sc[r:P:16, :].bitcast(I32), by_row[r])
+        load_ws_rows(0)
+        load_ws_rows(1)
         nc.sync.dma_start(tab0[:], words(tab_words[0]))
-        nc.sync.dma_start(ws[:, 0 : 2 * R].bitcast(I32), ws_words[0].bitcast(I32))
-        load_planes(ws_scales, 0)
-        nc.sync.dma_start(wt[:, 0:R].bitcast(I32), words(wt_words[0]))
+        nc.sync.dma_start(
+            ws[:].bitcast(I32).rearrange("p (a w) -> p a w", a=2), ws_words.bitcast(I32).rearrange("a p w -> p a w")
+        )
+        load_ws_rows(2)
+        load_ws_rows(3)
         nc.sync.dma_start(tab1[:], words(tab_words[1]))
+        nc.sync.dma_start(wt[:, 0:R].bitcast(I32), words(wt_words[0]))
         for q in range(4):
             nc.sync.dma_start(
                 w_sc[32 * q : 32 * q + 8, 2 * R : 3 * R].bitcast(I32), wt_scales[:, 4 * q : 4 * q + 4, :].bitcast(I32)
             )
         nc.sync.dma_start(wt[:, R : 2 * R].bitcast(I32), words(wt_words[1]))
-        nc.sync.dma_start(ws[:, 2 * R : 4 * R].bitcast(I32), ws_words[1].bitcast(I32))
         nc.vector.tensor_copy(sc0[:, 0:J], tab_sc[:].indirect(src_list[:]))
         nc.vector.tensor_copy(sc0[:, J : 2 * J], tab_sc[:].indirect(dst_list[:]))
         sc1 = keep.tile([P, 2 * J], U8, name="sc1", tag="tab_sc", align_bytes=64)
@@ -172,6 +173,7 @@ def tile_list_msg_relu_bias_kernel(
         for g in range(2):
             s0.append(word_tile("s0_%d" % g, "s0_%d" % g, quarter))
             gather_words(s0[g][:], tab0, src_list, g * quarter, (g + 1) * quarter)
+        for g in range(2):
             d0.append(word_tile("d0_%d" % g, "d0_%d" % g, quarter))
             gather_words(d0[g][:], tab0, dst_list, g * quarter, (g + 1) * quarter)
         for g in range(2):
@@ -179,8 +181,8 @@ def tile_list_msg_relu_bias_kernel(
             gather_words(d1[g][:], tab1, dst_list, g * quarter, (g + 1) * quarter)
             s1.append(word_tile("s1_%d" % g, "s1_%d" % g, quarter))
             gather_words(s1[g][:], tab1, src_list, g * quarter, (g + 1) * quarter)
-        for g in range(2):
-            for i, picked in ((0, s0), (1, d0)):
+        for i, picked in ((0, s0), (1, d0)):
+            for g in range(2):
                 for jt in range(2):
                     mx_pass(2 * g + jt, i, cols(picked[g], jt))
         ident = keep.tile([P, P], F32, name="ident", tag="s0_0", align_bytes=64)

@@ -29,62 +29,78 @@ def tile_list_msg_relu_bias_kernel(
     nc = tc.nc
     with ExitStack() as ctx:
         keep = ctx.enter_context(tc.tile_pool(name="keep", bufs=1))
+        laid = ctx.enter_context(tc.tile_pool(name="laid", bufs=1))
         psum = ctx.enter_context(tc.psum_pool(name="psum", bufs=1))
 
         src_list = keep.tile([P, J // 16], U16, name="src_list")
         dst_list = keep.tile([P, J // 16], U16, name="dst_list")
         tab0 = keep.tile([P, T], I32, name="tab0", align_bytes=64)
         tab1 = keep.tile([P, T], I32, name="tab1", align_bytes=64)
-        tab_sc = keep.tile([P, T], U8, name="tab_sc", tag="tab_sc", align_bytes=64)
+        tab_sc = laid.tile([P, T], U8, name="tab_sc", offset=0, align_bytes=64)
         ws = keep.tile([P, 2 * 2 * R], U8, name="ws", align_bytes=64)
+        ws_sc = keep.tile([P, 2 * R], U8, name="ws_sc", align_bytes=64)
+        wt_sc = keep.tile([P, 2 * R], U8, name="wt_sc", align_bytes=64)
+        src_rows = keep.tile([P, J], U8, name="src_rows", align_bytes=64)
+        dst_rows = keep.tile([P, J], U8, name="dst_rows", align_bytes=64)
         wt = keep.tile([P, 2 * R], U32, name="wt", align_bytes=64)
-        w_sc = keep.tile([P, 3 * R], U8, name="w_sc", align_bytes=64)
-        sc0 = keep.tile([P, 2 * J], U8, name="sc0", align_bytes=64)
         wd = keep.tile([P, N], U32, name="wd", align_bytes=64)
+        wd_sc = keep.tile([P, N], U8, name="wd_sc", align_bytes=64)
         weight = keep.tile([P, J], F32, name="weight")
         bias = keep.tile([P, N // P], F32, name="bias")
+        src_sc = keep.tile([P, 2 * J], U8, name="src_sc", align_bytes=64)
+        dst_sc = keep.tile([P, 2 * J], U8, name="dst_sc", align_bytes=64)
         page_a = keep.tile([P, T], F32, name="page_a")
-        page_b = keep.tile([P, T], F32, name="page_b")
         bank = [psum.tile([P, R], F32, name="bank%d" % i) for i in range(8)]
 
-        nc.vector.memset(tab_sc[:].bitcast(I32), 0)
+        nc.vector.memset(tab_sc[0:96, :].bitcast(I32), 0)
         nc.vector.memset(page_a[:].bitcast(I32), 0)
-        nc.vector.memset(page_b[:].bitcast(I32), 0)
 
         def words(ap):
             return ap.rearrange("p t i -> p (t i)").bitcast(I32)
 
-        def load_ws_rows(q):
+        def load_rows(plane, scales, q):
             nc.sync.dma_start(
-                w_sc[32 * q : 32 * q + 4, 0 : 2 * R].bitcast(I32).rearrange("p (a w) -> p a w", a=2),
-                ws_scales[:, 4 * q : 4 * q + 4, :].bitcast(I32).rearrange("a r w -> r a w"),
+                plane[32 * q : 32 * q + 4, :].bitcast(I32).rearrange("p (a w) -> p a w", a=2),
+                scales[:, 4 * q : 4 * q + 4, :].bitcast(I32).rearrange("a r w -> r a w"),
             )
 
+        def move_rows(queue, plane, rows):
+            for q in range(4):
+                queue.dma_start(
+                    plane[32 * q : 32 * q + 4, :].bitcast(I32).rearrange("p (a w) -> p a w", a=2),
+                    rows[96 + 8 * q : 96 + 8 * q + 8, :].bitcast(I32),
+                )
+
+        nc.sync.dma_start(tab_sc[96:P, :].bitcast(I32), tab_scales.bitcast(I32).rearrange("a s w -> s a w"))
         nc.sync.dma_start(src_list[:], offs)
         nc.sync.dma_start(dst_list[:], offs2)
-        by_row = tab_scales.bitcast(I32).rearrange("a (q r) w -> r q a w", r=4)
-        for r in range(4):
-            nc.sync.dma_start(tab_sc[r:P:16, :].bitcast(I32), by_row[r])
-        load_ws_rows(0)
-        load_ws_rows(1)
+        load_rows(ws_sc, ws_scales, 0)
         nc.sync.dma_start(tab0[:], words(tab_words[0]))
         nc.sync.dma_start(
             ws[:].bitcast(I32).rearrange("p (a w) -> p a w", a=2), ws_words.bitcast(I32).rearrange("a p w -> p a w")
         )
-        load_ws_rows(2)
-        load_ws_rows(3)
+        for q in range(1, 4):
+            load_rows(ws_sc, ws_scales, q)
+        for q in range(2):
+            load_rows(wt_sc, wt_scales, q)
         nc.sync.dma_start(tab1[:], words(tab_words[1]))
-        nc.sync.dma_start(wt[:, 0:R].bitcast(I32), words(wt_words[0]))
-        for q in range(4):
-            nc.sync.dma_start(
-                w_sc[32 * q : 32 * q + 8, 2 * R : 3 * R].bitcast(I32), wt_scales[:, 4 * q : 4 * q + 4, :].bitcast(I32)
-            )
-        nc.sync.dma_start(wt[:, R : 2 * R].bitcast(I32), words(wt_words[1]))
-        nc.vector.tensor_copy(sc0[:, 0:J], tab_sc[:].indirect(src_list[:]))
-        nc.vector.tensor_copy(sc0[:, J : 2 * J], tab_sc[:].indirect(dst_list[:]))
-        sc1 = keep.tile([P, 2 * J], U8, name="sc1", tag="tab_sc", align_bytes=64)
-        nc.sync.dma_start(sc1[0 : P - 16, :].bitcast(I32), sc0[16:P, :].bitcast(I32))
+        for q in range(2, 4):
+            load_rows(wt_sc, wt_scales, q)
+        nc.vector.tensor_copy(src_rows[:], tab_sc[:].indirect(src_list[:]))
+        move_rows(nc.sync, src_sc, src_rows)
+        nc.sync.dma_start(
+            wt[:].bitcast(I32).rearrange("p (a w) -> p a w", a=2),
+            wt_words.rearrange("a p t i -> p a (t i)").bitcast(I32),
+        )
+        nc.vector.tensor_copy(dst_rows[:], tab_sc[:].indirect(dst_list[:]))
+        move_rows(nc.sync, dst_sc, dst_rows)
+        ident = laid.tile([P, P], F32, name="ident", offset=0, align_bytes=64)
+        page_b = laid.tile([P, T], F32, name="page_b", offset=512, align_bytes=64)
+        make_identity(nc, ident[:])
+        nc.gpsimd.memset(page_b[:], 0.0)
         nc.sync.dma_start(wd[:].bitcast(I32), words(wd_words[0]))
+        for q in range(4):
+            nc.sync.dma_start(wd_sc[32 * q : 32 * q + 4, :].bitcast(I32), wd_scales[0, 4 * q : 4 * q + 4, :].bitcast(I32))
         with nc.allow_non_contiguous_dma(reason="one bias value a partition"):
             nc.sync.dma_start(bias[:], b.rearrange("(m p) -> p m", p=P))
         nc.sync.dma_start(weight[:], wgo)
@@ -99,13 +115,13 @@ def tile_list_msg_relu_bias_kernel(
             return keep.tile([P, width], U32, name=name, tag=tag, align_bytes=64)
 
         def mx_pass(jt, i, picked, first=0, last=3):
-            src = slice(jt * P, (jt + 1) * P)
-            dst = slice(J + jt * P, J + (jt + 1) * P)
+            pass0 = slice(jt * P, (jt + 1) * P)
+            pass1 = slice(J + jt * P, J + (jt + 1) * P)
             plane, w, w_plane = (
-                (sc0[:, src], ws[:, 0 : 2 * R].bitcast(FP4X4), w_sc[:, 0:R]),
-                (sc0[:, dst], wt[:, 0:R].bitcast(FP8X4), w_sc[:, 2 * R : 3 * R]),
-                (sc1[:, dst], wt[:, R : 2 * R].bitcast(FP8X4), w_sc[4:P, 2 * R : 3 * R]),
-                (sc1[:, src], ws[:, 2 * R : 4 * R].bitcast(FP4X4), w_sc[:, R : 2 * R]),
+                (src_sc[:, pass0], ws[:, 0 : 2 * R].bitcast(FP4X4), ws_sc[:, 0:R]),
+                (dst_sc[:, pass0], wt[:, 0:R].bitcast(FP8X4), wt_sc[:, 0:R]),
+                (dst_sc[:, pass1], wt[:, R : 2 * R].bitcast(FP8X4), wt_sc[:, R : 2 * R]),
+                (src_sc[:, pass1], ws[:, 2 * R : 4 * R].bitcast(FP4X4), ws_sc[:, R : 2 * R]),
             )[i]
             nc.tensor.matmul_mx(
                 bank[jt][:],
@@ -177,35 +193,34 @@ def tile_list_msg_relu_bias_kernel(
             d0.append(word_tile("d0_%d" % g, "d0_%d" % g, quarter))
             gather_words(d0[g][:], tab0, dst_list, g * quarter, (g + 1) * quarter)
         for g in range(2):
-            d1.append(word_tile("d1_%d" % g, "d1_%d" % g, quarter))
-            gather_words(d1[g][:], tab1, dst_list, g * quarter, (g + 1) * quarter)
             s1.append(word_tile("s1_%d" % g, "s1_%d" % g, quarter))
             gather_words(s1[g][:], tab1, src_list, g * quarter, (g + 1) * quarter)
-        for i, picked in ((0, s0), (1, d0)):
-            for g in range(2):
-                for jt in range(2):
-                    mx_pass(2 * g + jt, i, cols(picked[g], jt))
-        ident = keep.tile([P, P], F32, name="ident", tag="s0_0", align_bytes=64)
-        make_identity(nc, ident[:])
-        wd_sc = keep.tile([P, N], U8, name="wd_sc", tag="d0_0", align_bytes=64)
-        for q in range(4):
-            nc.sync.dma_start(wd_sc[32 * q : 32 * q + 4, :].bitcast(I32), wd_scales[0, 4 * q : 4 * q + 4, :].bitcast(I32))
+            d1.append(word_tile("d1_%d" % g, "d1_%d" % g, quarter))
+            gather_words(d1[g][:], tab1, dst_list, g * quarter, (g + 1) * quarter)
+        for g in range(2):
+            for jt in range(2):
+                mx_pass(2 * g + jt, 0, cols(s0[g], jt))
         h = [
             keep.tile([P, 4 * quarter], BF16, name="h_0", tag="h_0", align_bytes=64),
             keep.tile([P, 4 * quarter], BF16, name="h_1", tag="h_1", align_bytes=64),
         ]
-        for g in range(2):
-            for jt in range(2):
-                mx_pass(2 * g + jt, 2, cols(d1[g], jt))
-                mx_pass(2 * g + jt, 3, cols(s1[g], jt))
-            hidden(h[g], (2 * g, 2 * g + 1))
+        for jt in range(2):
+            mx_pass(jt, 3, cols(s1[0], jt), 0, 2)
+        for jt in range(2):
+            mx_pass(jt, 1, cols(d0[0], jt), 0, 2)
+            mx_pass(jt, 2, cols(d1[0], jt), 0, 2)
+        hidden(h[0], (0, 1))
+        for jt in range(2):
+            for i, picked in ((1, d0), (2, d1), (3, s1)):
+                mx_pass(2 + jt, i, cols(picked[1], jt))
+        hidden(h[1], (2, 3))
 
 
         d1 = word_tile("d1_y", "d1_y", HALF)
         gather_words(d1[:], tab1, dst_list, HALF, J)
         s1 = word_tile("s1_y", "s1_y", HALF)
         gather_words(s1[:], tab1, src_list, HALF, J)
-        s0 = word_tile("s0_y", "d1_0", HALF)
+        s0 = word_tile("s0_y", "s1_0", HALF)
         gather_words(s0[:], tab0, src_list, HALF, J)
         hq_a = quantise(h[0], "hq_a", "hq_a")
         d0 = word_tile("d0_y", "h_0", HALF)

@@ -41,12 +41,8 @@ def tile_list_msg_relu_bias_kernel(
         ws_sc = keep.tile([P, 2 * R], U8, name="ws_sc", align_bytes=64)
         wt_sc = keep.tile([P, 2 * R], U8, name="wt_sc", align_bytes=64)
         src_rows = keep.tile([P, J], U8, name="src_rows", align_bytes=64)
-        dst_rows = keep.tile([P, J], U8, name="dst_rows", align_bytes=64)
+        dst_rows = laid.tile([P, J], U8, name="dst_rows", offset=10496, align_bytes=64)
         wt = keep.tile([P, 2 * R], U32, name="wt", align_bytes=64)
-        wd = keep.tile([P, N], U32, name="wd", align_bytes=64)
-        wd_sc = keep.tile([P, N], U8, name="wd_sc", align_bytes=64)
-        weight = keep.tile([P, J], F32, name="weight")
-        bias = keep.tile([P, N // P], F32, name="bias")
         src_sc = keep.tile([P, 2 * J], U8, name="src_sc", align_bytes=64)
         dst_sc = keep.tile([P, 2 * J], U8, name="dst_sc", align_bytes=64)
         page_a = keep.tile([P, T], F32, name="page_a")
@@ -58,49 +54,53 @@ def tile_list_msg_relu_bias_kernel(
         def words(ap):
             return ap.rearrange("p t i -> p (t i)").bitcast(I32)
 
-        def load_rows(plane, scales, q):
+        def load_rows(plane, first, scales, r):
             nc.sync.dma_start(
-                plane[32 * q : 32 * q + 4, :].bitcast(I32).rearrange("p (a w) -> p a w", a=2),
-                scales[:, 4 * q : 4 * q + 4, :].bitcast(I32).rearrange("a r w -> r a w"),
+                plane[first + r : P : 32, :].bitcast(I32).rearrange("p (a w) -> p a w", a=scales.shape[0]),
+                scales.bitcast(I32).rearrange("a (q r) w -> r q a w", r=4)[r],
             )
 
-        def move_rows(queue, plane, rows):
-            for q in range(4):
-                queue.dma_start(
-                    plane[32 * q : 32 * q + 4, :].bitcast(I32).rearrange("p (a w) -> p a w", a=2),
+        def move_rows(plane, first, rows):
+            for q in (0, 2, 1, 3):
+                nc.sync.dma_start(
+                    plane[32 * q + first : 32 * q + first + 4, :].bitcast(I32).rearrange("p (a w) -> p a w", a=2),
                     rows[96 + 8 * q : 96 + 8 * q + 8, :].bitcast(I32),
                 )
 
         nc.sync.dma_start(tab_sc[96:P, :].bitcast(I32), tab_scales.bitcast(I32).rearrange("a s w -> s a w"))
         nc.sync.dma_start(src_list[:], offs)
         nc.sync.dma_start(dst_list[:], offs2)
-        load_rows(ws_sc, ws_scales, 0)
+        load_rows(ws_sc, 0, ws_scales, 0)
         nc.sync.dma_start(tab0[:], words(tab_words[0]))
         nc.sync.dma_start(
             ws[:].bitcast(I32).rearrange("p (a w) -> p a w", a=2), ws_words.bitcast(I32).rearrange("a p w -> p a w")
         )
         for q in range(1, 4):
-            load_rows(ws_sc, ws_scales, q)
+            load_rows(ws_sc, 0, ws_scales, q)
         for q in range(2):
-            load_rows(wt_sc, wt_scales, q)
+            load_rows(wt_sc, 4, wt_scales, q)
         nc.sync.dma_start(tab1[:], words(tab_words[1]))
         for q in range(2, 4):
-            load_rows(wt_sc, wt_scales, q)
+            load_rows(wt_sc, 4, wt_scales, q)
         nc.vector.tensor_copy(src_rows[:], tab_sc[:].indirect(src_list[:]))
-        move_rows(nc.sync, src_sc, src_rows)
+        move_rows(src_sc, 0, src_rows)
         nc.sync.dma_start(
             wt[:].bitcast(I32).rearrange("p (a w) -> p a w", a=2),
             wt_words.rearrange("a p t i -> p a (t i)").bitcast(I32),
         )
         nc.vector.tensor_copy(dst_rows[:], tab_sc[:].indirect(dst_list[:]))
-        move_rows(nc.sync, dst_sc, dst_rows)
+        move_rows(dst_sc, 8, dst_rows)
         ident = laid.tile([P, P], F32, name="ident", offset=0, align_bytes=64)
         page_b = laid.tile([P, T], F32, name="page_b", offset=512, align_bytes=64)
+        wd = laid.tile([P, N], U32, name="wd", offset=8704, align_bytes=64)
+        wd_sc = laid.tile([P, N], U8, name="wd_sc", offset=10752, align_bytes=64)
+        bias = laid.tile([P, N // P], F32, name="bias", offset=11264, align_bytes=64)
+        weight = laid.tile([P, J], F32, name="weight", offset=11328, align_bytes=64)
         make_identity(nc, ident[:])
         nc.gpsimd.memset(page_b[:], 0.0)
         nc.sync.dma_start(wd[:].bitcast(I32), words(wd_words[0]))
         for q in range(4):
-            nc.sync.dma_start(wd_sc[32 * q : 32 * q + 4, :].bitcast(I32), wd_scales[0, 4 * q : 4 * q + 4, :].bitcast(I32))
+            load_rows(wd_sc, 0, wd_scales, q)
         with nc.allow_non_contiguous_dma(reason="one bias value a partition"):
             nc.sync.dma_start(bias[:], b.rearrange("(m p) -> p m", p=P))
         nc.sync.dma_start(weight[:], wgo)
@@ -119,8 +119,8 @@ def tile_list_msg_relu_bias_kernel(
             pass1 = slice(J + jt * P, J + (jt + 1) * P)
             plane, w, w_plane = (
                 (src_sc[:, pass0], ws[:, 0 : 2 * R].bitcast(FP4X4), ws_sc[:, 0:R]),
-                (dst_sc[:, pass0], wt[:, 0:R].bitcast(FP8X4), wt_sc[:, 0:R]),
-                (dst_sc[:, pass1], wt[:, R : 2 * R].bitcast(FP8X4), wt_sc[:, R : 2 * R]),
+                (dst_sc[8:P, pass0], wt[:, 0:R].bitcast(FP8X4), wt_sc[4:P, 0:R]),
+                (dst_sc[8:P, pass1], wt[:, R : 2 * R].bitcast(FP8X4), wt_sc[4:P, R : 2 * R]),
                 (src_sc[:, pass1], ws[:, 2 * R : 4 * R].bitcast(FP4X4), ws_sc[:, R : 2 * R]),
             )[i]
             nc.tensor.matmul_mx(

@@ -40,11 +40,13 @@ def tile_list_msg_relu_bias_kernel(
         ws = keep.tile([P, 2 * 2 * R], U8, name="ws", align_bytes=64)
         ws_sc = keep.tile([P, 2 * R], U8, name="ws_sc", align_bytes=64)
         wt_sc = keep.tile([P, 2 * R], U8, name="wt_sc", align_bytes=64)
-        src_rows = keep.tile([P, J], U8, name="src_rows", align_bytes=64)
-        dst_rows = laid.tile([P, J], U8, name="dst_rows", offset=10496, align_bytes=64)
+        rows = [keep.tile([P, 2 * HALF], U8, name="rows%d" % g, align_bytes=64) for g in range(2)]
+        planes = [keep.tile([P, 4 * HALF], U8, name="planes%d" % g, align_bytes=64) for g in range(2)]
         wt = keep.tile([P, 2 * R], U32, name="wt", align_bytes=64)
-        src_sc = keep.tile([P, 2 * J], U8, name="src_sc", align_bytes=64)
-        dst_sc = keep.tile([P, 2 * J], U8, name="dst_sc", align_bytes=64)
+        wd = keep.tile([P, N], U32, name="wd", align_bytes=64)
+        wd_sc = keep.tile([P, N], U8, name="wd_sc", align_bytes=64)
+        weight = keep.tile([P, J], F32, name="weight")
+        bias = keep.tile([P, N // P], F32, name="bias")
         page_a = keep.tile([P, T], F32, name="page_a")
         bank = [psum.tile([P, R], F32, name="bank%d" % i) for i in range(8)]
 
@@ -60,16 +62,23 @@ def tile_list_msg_relu_bias_kernel(
                 scales.bitcast(I32).rearrange("a (q r) w -> r q a w", r=4)[r],
             )
 
-        def move_rows(plane, first, rows):
+        def entries(lst, lo, hi):
+            return lst[:, lo // 16 : hi // 16]
+
+        def gather_planes(g):
+            for k, lst in enumerate((src_list, dst_list)):
+                nc.vector.tensor_copy(
+                    rows[g][:, k * HALF : (k + 1) * HALF], tab_sc[:].indirect(entries(lst, g * HALF, (g + 1) * HALF))
+                )
             for q in (0, 2, 1, 3):
                 nc.sync.dma_start(
-                    plane[32 * q + first : 32 * q + first + 4, :].bitcast(I32).rearrange("p (a w) -> p a w", a=2),
-                    rows[96 + 8 * q : 96 + 8 * q + 8, :].bitcast(I32),
+                    planes[g][32 * q : 32 * q + 4, :].bitcast(I32).rearrange("p (a w) -> p a w", a=2),
+                    rows[g][96 + 8 * q : 96 + 8 * q + 8, :].bitcast(I32),
                 )
 
-        nc.sync.dma_start(tab_sc[96:P, :].bitcast(I32), tab_scales.bitcast(I32).rearrange("a s w -> s a w"))
         nc.sync.dma_start(src_list[:], offs)
         nc.sync.dma_start(dst_list[:], offs2)
+        nc.sync.dma_start(tab_sc[96:P, :].bitcast(I32), tab_scales.bitcast(I32).rearrange("a s w -> s a w"))
         load_rows(ws_sc, 0, ws_scales, 0)
         nc.sync.dma_start(tab0[:], words(tab_words[0]))
         nc.sync.dma_start(
@@ -80,22 +89,16 @@ def tile_list_msg_relu_bias_kernel(
         for q in range(2):
             load_rows(wt_sc, 4, wt_scales, q)
         nc.sync.dma_start(tab1[:], words(tab_words[1]))
+        gather_planes(0)
         for q in range(2, 4):
             load_rows(wt_sc, 4, wt_scales, q)
-        nc.vector.tensor_copy(src_rows[:], tab_sc[:].indirect(src_list[:]))
-        move_rows(src_sc, 0, src_rows)
         nc.sync.dma_start(
             wt[:].bitcast(I32).rearrange("p (a w) -> p a w", a=2),
             wt_words.rearrange("a p t i -> p a (t i)").bitcast(I32),
         )
-        nc.vector.tensor_copy(dst_rows[:], tab_sc[:].indirect(dst_list[:]))
-        move_rows(dst_sc, 8, dst_rows)
+        gather_planes(1)
         ident = laid.tile([P, P], F32, name="ident", offset=0, align_bytes=64)
         page_b = laid.tile([P, T], F32, name="page_b", offset=512, align_bytes=64)
-        wd = laid.tile([P, N], U32, name="wd", offset=8704, align_bytes=64)
-        wd_sc = laid.tile([P, N], U8, name="wd_sc", offset=10752, align_bytes=64)
-        bias = laid.tile([P, N // P], F32, name="bias", offset=11264, align_bytes=64)
-        weight = laid.tile([P, J], F32, name="weight", offset=11328, align_bytes=64)
         make_identity(nc, ident[:])
         nc.gpsimd.memset(page_b[:], 0.0)
         nc.sync.dma_start(wd[:].bitcast(I32), words(wd_words[0]))
@@ -105,9 +108,6 @@ def tile_list_msg_relu_bias_kernel(
             nc.sync.dma_start(bias[:], b.rearrange("(m p) -> p m", p=P))
         nc.sync.dma_start(weight[:], wgo)
 
-        def entries(lst, lo, hi):
-            return lst[:, lo // 16 : hi // 16]
-
         def gather_words(picked, tab, lst, lo, hi):
             nc.vector.tensor_copy(picked, tab[:].bitcast(U32).indirect(entries(lst, lo, hi)))
 
@@ -115,13 +115,15 @@ def tile_list_msg_relu_bias_kernel(
             return keep.tile([P, width], U32, name=name, tag=tag, align_bytes=64)
 
         def mx_pass(jt, i, picked, first=0, last=3):
-            pass0 = slice(jt * P, (jt + 1) * P)
-            pass1 = slice(J + jt * P, J + (jt + 1) * P)
+            def picked_plane(a, k):
+                lo = (2 * a + k) * HALF + (jt % TILES) * P
+                return planes[jt // TILES][:, lo : lo + P]
+
             plane, w, w_plane = (
-                (src_sc[:, pass0], ws[:, 0 : 2 * R].bitcast(FP4X4), ws_sc[:, 0:R]),
-                (dst_sc[8:P, pass0], wt[:, 0:R].bitcast(FP8X4), wt_sc[4:P, 0:R]),
-                (dst_sc[8:P, pass1], wt[:, R : 2 * R].bitcast(FP8X4), wt_sc[4:P, R : 2 * R]),
-                (src_sc[:, pass1], ws[:, 2 * R : 4 * R].bitcast(FP4X4), ws_sc[:, R : 2 * R]),
+                (picked_plane(0, 0), ws[:, 0 : 2 * R].bitcast(FP4X4), ws_sc[:, 0:R]),
+                (picked_plane(0, 1), wt[:, 0:R].bitcast(FP8X4), wt_sc[4:P, 0:R]),
+                (picked_plane(1, 1), wt[:, R : 2 * R].bitcast(FP8X4), wt_sc[4:P, R : 2 * R]),
+                (picked_plane(1, 0), ws[:, 2 * R : 4 * R].bitcast(FP4X4), ws_sc[:, R : 2 * R]),
             )[i]
             nc.tensor.matmul_mx(
                 bank[jt][:],
@@ -193,10 +195,10 @@ def tile_list_msg_relu_bias_kernel(
             d0.append(word_tile("d0_%d" % g, "d0_%d" % g, quarter))
             gather_words(d0[g][:], tab0, dst_list, g * quarter, (g + 1) * quarter)
         for g in range(2):
-            s1.append(word_tile("s1_%d" % g, "s1_%d" % g, quarter))
-            gather_words(s1[g][:], tab1, src_list, g * quarter, (g + 1) * quarter)
             d1.append(word_tile("d1_%d" % g, "d1_%d" % g, quarter))
             gather_words(d1[g][:], tab1, dst_list, g * quarter, (g + 1) * quarter)
+            s1.append(word_tile("s1_%d" % g, "s1_%d" % g, quarter))
+            gather_words(s1[g][:], tab1, src_list, g * quarter, (g + 1) * quarter)
         for g in range(2):
             for jt in range(2):
                 mx_pass(2 * g + jt, 0, cols(s0[g], jt))
@@ -204,23 +206,18 @@ def tile_list_msg_relu_bias_kernel(
             keep.tile([P, 4 * quarter], BF16, name="h_0", tag="h_0", align_bytes=64),
             keep.tile([P, 4 * quarter], BF16, name="h_1", tag="h_1", align_bytes=64),
         ]
-        for jt in range(2):
-            mx_pass(jt, 3, cols(s1[0], jt), 0, 2)
-        for jt in range(2):
-            mx_pass(jt, 1, cols(d0[0], jt), 0, 2)
-            mx_pass(jt, 2, cols(d1[0], jt), 0, 2)
-        hidden(h[0], (0, 1))
-        for jt in range(2):
+        for g in range(2):
             for i, picked in ((1, d0), (2, d1), (3, s1)):
-                mx_pass(2 + jt, i, cols(picked[1], jt))
-        hidden(h[1], (2, 3))
+                for jt in range(2):
+                    mx_pass(2 * g + jt, i, cols(picked[g], jt))
+            hidden(h[g], (2 * g, 2 * g + 1))
 
 
         d1 = word_tile("d1_y", "d1_y", HALF)
         gather_words(d1[:], tab1, dst_list, HALF, J)
         s1 = word_tile("s1_y", "s1_y", HALF)
         gather_words(s1[:], tab1, src_list, HALF, J)
-        s0 = word_tile("s0_y", "s1_0", HALF)
+        s0 = word_tile("s0_y", "d1_0", HALF)
         gather_words(s0[:], tab0, src_list, HALF, J)
         hq_a = quantise(h[0], "hq_a", "hq_a")
         d0 = word_tile("d0_y", "h_0", HALF)

@@ -81,9 +81,7 @@ def tile_list_msg_relu_bias_kernel(
         nc.sync.dma_start(tab_sc[96:P, :].bitcast(I32), tab_scales.bitcast(I32).rearrange("a s w -> s a w"))
         load_rows(ws_sc, 0, ws_scales, 0)
         nc.sync.dma_start(tab0[:], words(tab_words[0]))
-        nc.sync.dma_start(
-            ws[:].bitcast(I32).rearrange("p (a w) -> p a w", a=2), ws_words.bitcast(I32).rearrange("a p w -> p a w")
-        )
+        nc.sync.dma_start(ws[:, 0 : 2 * R].bitcast(I32), ws_words[0].bitcast(I32))
         for q in range(1, 4):
             load_rows(ws_sc, 0, ws_scales, q)
         for q in range(2):
@@ -96,6 +94,7 @@ def tile_list_msg_relu_bias_kernel(
             wt[:].bitcast(I32).rearrange("p (a w) -> p a w", a=2),
             wt_words.rearrange("a p t i -> p a (t i)").bitcast(I32),
         )
+        nc.sync.dma_start(ws[:, 2 * R : 4 * R].bitcast(I32), ws_words[1].bitcast(I32))
         gather_planes(1)
         ident = laid.tile([P, P], F32, name="ident", offset=0, align_bytes=64)
         page_b = laid.tile([P, T], F32, name="page_b", offset=512, align_bytes=64)
@@ -191,9 +190,9 @@ def tile_list_msg_relu_bias_kernel(
         for g in range(2):
             s0.append(word_tile("s0_%d" % g, "s0_%d" % g, quarter))
             gather_words(s0[g][:], tab0, src_list, g * quarter, (g + 1) * quarter)
-        for g in range(2):
-            d0.append(word_tile("d0_%d" % g, "d0_%d" % g, quarter))
-            gather_words(d0[g][:], tab0, dst_list, g * quarter, (g + 1) * quarter)
+        d0_half = word_tile("d0", "d0", HALF)
+        gather_words(d0_half[:], tab0, dst_list, 0, HALF)
+        d0 = [d0_half[:, g * quarter : (g + 1) * quarter] for g in range(2)]
         for g in range(2):
             d1.append(word_tile("d1_%d" % g, "d1_%d" % g, quarter))
             gather_words(d1[g][:], tab1, dst_list, g * quarter, (g + 1) * quarter)

@@ -29,14 +29,13 @@ def tile_list_msg_relu_bias_kernel(
     nc = tc.nc
     with ExitStack() as ctx:
         keep = ctx.enter_context(tc.tile_pool(name="keep", bufs=1))
-        laid = ctx.enter_context(tc.tile_pool(name="laid", bufs=1))
         psum = ctx.enter_context(tc.psum_pool(name="psum", bufs=1))
 
         src_list = keep.tile([P, J // 16], U16, name="src_list")
         dst_list = keep.tile([P, J // 16], U16, name="dst_list")
         tab0 = keep.tile([P, T], I32, name="tab0", align_bytes=64)
         tab1 = keep.tile([P, T], I32, name="tab1", align_bytes=64)
-        tab_sc = laid.tile([P, T], U8, name="tab_sc", offset=0, align_bytes=64)
+        tab_sc = keep.tile([P, T], U8, name="tab_sc", tag="tab_sc", align_bytes=64)
         ws = keep.tile([P, 2 * 2 * R], U8, name="ws", align_bytes=64)
         ws_sc = keep.tile([P, 2 * R], U8, name="ws_sc", align_bytes=64)
         wt_sc = keep.tile([P, 2 * R], U8, name="wt_sc", align_bytes=64)
@@ -50,6 +49,8 @@ def tile_list_msg_relu_bias_kernel(
         page_a = keep.tile([P, T], F32, name="page_a")
         bank = [psum.tile([P, R], F32, name="bank%d" % i) for i in range(8)]
 
+        ident = keep.tile([P, P], F32, name="ident", align_bytes=64)
+        make_identity(nc, ident[:])
         nc.vector.memset(tab_sc[0:96, :].bitcast(I32), 0)
         nc.vector.memset(page_a[:].bitcast(I32), 0)
 
@@ -96,9 +97,7 @@ def tile_list_msg_relu_bias_kernel(
         )
         nc.sync.dma_start(ws[:, 2 * R : 4 * R].bitcast(I32), ws_words[1].bitcast(I32))
         gather_planes(1)
-        ident = laid.tile([P, P], F32, name="ident", offset=0, align_bytes=64)
-        page_b = laid.tile([P, T], F32, name="page_b", offset=512, align_bytes=64)
-        make_identity(nc, ident[:])
+        page_b = keep.tile([P, T], F32, name="page_b", tag="tab_sc", align_bytes=64)
         nc.gpsimd.memset(page_b[:], 0.0)
         nc.sync.dma_start(wd[:].bitcast(I32), words(wd_words[0]))
         for q in range(4):

@@ -1,7 +1,6 @@
 from contextlib import ExitStack
 
 import concourse.mybir as mybir
-from concourse.masks import make_identity
 
 K, R, N, T, J = 1024, 512, 512, 2048, 1024
 FLOPS = 2 * (2 * K * R * J + R * N * J)
@@ -37,71 +36,73 @@ def tile_list_msg_relu_bias_kernel(
         tab1 = keep.tile([P, T], I32, name="tab1", align_bytes=64)
         tab_sc = keep.tile([P, T], U8, name="tab_sc", tag="tab_sc", align_bytes=64)
         ws = keep.tile([P, 2 * 2 * R], U8, name="ws", align_bytes=64)
-        ws_sc = keep.tile([P, 2 * R], U8, name="ws_sc", align_bytes=64)
-        wt_sc = keep.tile([P, 2 * R], U8, name="wt_sc", align_bytes=64)
-        rows = [keep.tile([P, 2 * HALF], U8, name="rows%d" % g, align_bytes=64) for g in range(2)]
+        w_sc = keep.tile([P, 5 * R], U8, name="w_sc", align_bytes=64)
+        rows = keep.tile([P, 2 * J], U8, name="rows", align_bytes=64)
         planes = [keep.tile([P, 4 * HALF], U8, name="planes%d" % g, align_bytes=64) for g in range(2)]
         wt = keep.tile([P, 2 * R], U32, name="wt", align_bytes=64)
-        wd = keep.tile([P, N], U32, name="wd", align_bytes=64)
-        wd_sc = keep.tile([P, N], U8, name="wd_sc", align_bytes=64)
+        wd_first = keep.tile([P, P], U32, name="wd_first", align_bytes=64)
+        wd_rest = keep.tile([P, N - P], U32, name="wd_rest", align_bytes=64)
+        wd = [wd_first[:]] + [wd_rest[:, m * P : (m + 1) * P] for m in range(N // P - 1)]
         weight = keep.tile([P, J], F32, name="weight")
         bias = keep.tile([P, N // P], F32, name="bias")
         page_a = keep.tile([P, T], F32, name="page_a")
         bank = [psum.tile([P, R], F32, name="bank%d" % i) for i in range(8)]
 
         ident = keep.tile([P, P], F32, name="ident", align_bytes=64)
-        make_identity(nc, ident[:])
+        apart = keep.tile([P, P], F32, name="apart")
+        nc.gpsimd.iota(apart[:], [[1, P]], base=0, channel_multiplier=-1, allow_small_or_imprecise_dtypes=True)
+        nc.scalar.activation(apart[:], apart[:], ACT.Abs)
+        nc.scalar.activation(ident[:], apart[:], ACT.Relu, bias=1.0, scale=-1.0)
         nc.vector.memset(tab_sc[0:96, :].bitcast(I32), 0)
         nc.vector.memset(page_a[:].bitcast(I32), 0)
 
         def words(ap):
             return ap.rearrange("p t i -> p (t i)").bitcast(I32)
 
-        def load_rows(plane, first, scales, r):
-            nc.sync.dma_start(
-                plane[first + r : P : 32, :].bitcast(I32).rearrange("p (a w) -> p a w", a=scales.shape[0]),
-                scales.bitcast(I32).rearrange("a (q r) w -> r q a w", r=4)[r],
-            )
+        def by_row(scales):
+            return scales.bitcast(I32).rearrange("a s w -> s a w")
 
         def entries(lst, lo, hi):
             return lst[:, lo // 16 : hi // 16]
 
-        def gather_planes(g):
-            for k, lst in enumerate((src_list, dst_list)):
-                nc.vector.tensor_copy(
-                    rows[g][:, k * HALF : (k + 1) * HALF], tab_sc[:].indirect(entries(lst, g * HALF, (g + 1) * HALF))
-                )
+        def target_planes(g):
+            nc.vector.tensor_copy(
+                rows[:, J + g * HALF : J + (g + 1) * HALF],
+                tab_sc[:].indirect(entries(dst_list, g * HALF, (g + 1) * HALF)),
+            )
             for q in (0, 2, 1, 3):
                 nc.sync.dma_start(
-                    planes[g][32 * q : 32 * q + 4, :].bitcast(I32).rearrange("p (a w) -> p a w", a=2),
-                    rows[g][96 + 8 * q : 96 + 8 * q + 8, :].bitcast(I32),
+                    planes[g][32 * q : 32 * q + 4, :].bitcast(I32).rearrange("p (a k w) -> p a k w", a=2, k=2),
+                    rows[96 + 8 * q : 96 + 8 * q + 8, :].bitcast(I32).rearrange("p (k g w) -> p g k w", k=2, g=2)[:, g],
                 )
 
+        nc.sync.dma_start(tab_sc[96:P, :].bitcast(I32), by_row(tab_scales))
         nc.sync.dma_start(src_list[:], offs)
         nc.sync.dma_start(dst_list[:], offs2)
-        nc.sync.dma_start(tab_sc[96:P, :].bitcast(I32), tab_scales.bitcast(I32).rearrange("a s w -> s a w"))
-        load_rows(ws_sc, 0, ws_scales, 0)
+        lo = 0
+        for scales in (ws_scales, wt_scales, wd_scales):
+            passes = scales.shape[0]
+            nc.sync.dma_start(
+                w_sc[0:16, lo : lo + passes * R].bitcast(I32).rearrange("p (a w) -> p a w", a=passes), by_row(scales)
+            )
+            lo = lo + passes * R
         nc.sync.dma_start(tab0[:], words(tab_words[0]))
         nc.sync.dma_start(ws[:, 0 : 2 * R].bitcast(I32), ws_words[0].bitcast(I32))
-        for q in range(1, 4):
-            load_rows(ws_sc, 0, ws_scales, q)
-        for q in range(2):
-            load_rows(wt_sc, 4, wt_scales, q)
+        nc.sync.dma_start(wd_first[:].bitcast(I32), words(wd_words[0])[:, 0:P])
+        for q in (2, 1, 3):
+            nc.sync.dma_start(w_sc[32 * q : 32 * q + 4, :].bitcast(I32), w_sc[4 * q : 4 * q + 4, :].bitcast(I32))
         nc.sync.dma_start(tab1[:], words(tab_words[1]))
-        gather_planes(0)
-        for q in range(2, 4):
-            load_rows(wt_sc, 4, wt_scales, q)
+        nc.vector.tensor_copy(rows[:, 0:J], tab_sc[:].indirect(src_list[:]))
+        target_planes(0)
         nc.sync.dma_start(
             wt[:].bitcast(I32).rearrange("p (a w) -> p a w", a=2),
             wt_words.rearrange("a p t i -> p a (t i)").bitcast(I32),
         )
         nc.sync.dma_start(ws[:, 2 * R : 4 * R].bitcast(I32), ws_words[1].bitcast(I32))
-        gather_planes(1)
+        target_planes(1)
         page_b = keep.tile([P, T], F32, name="page_b", tag="tab_sc", align_bytes=64)
         nc.gpsimd.memset(page_b[:], 0.0)
-        nc.sync.dma_start(wd[:].bitcast(I32), words(wd_words[0]))
-        for q in range(4):
-            load_rows(wd_sc, 0, wd_scales, q)
+        nc.sync.dma_start(wd_rest[:].bitcast(I32), words(wd_words[0])[:, P:N])
         with nc.allow_non_contiguous_dma(reason="one bias value a partition"):
             nc.sync.dma_start(bias[:], b.rearrange("(m p) -> p m", p=P))
         nc.sync.dma_start(weight[:], wgo)
@@ -118,10 +119,10 @@ def tile_list_msg_relu_bias_kernel(
                 return planes[jt // TILES][:, lo : lo + P]
 
             plane, w, w_plane = (
-                (picked_plane(0, 0), ws[:, 0 : 2 * R].bitcast(FP4X4), ws_sc[:, 0:R]),
-                (picked_plane(0, 1), wt[:, 0:R].bitcast(FP8X4), wt_sc[4:P, 0:R]),
-                (picked_plane(1, 1), wt[:, R : 2 * R].bitcast(FP8X4), wt_sc[4:P, R : 2 * R]),
-                (picked_plane(1, 0), ws[:, 2 * R : 4 * R].bitcast(FP4X4), ws_sc[:, R : 2 * R]),
+                (picked_plane(0, 0), ws[:, 0 : 2 * R].bitcast(FP4X4), w_sc[:, 0:R]),
+                (picked_plane(0, 1), wt[:, 0:R].bitcast(FP8X4), w_sc[:, 2 * R : 3 * R]),
+                (picked_plane(1, 1), wt[:, R : 2 * R].bitcast(FP8X4), w_sc[:, 3 * R : 4 * R]),
+                (picked_plane(1, 0), ws[:, 2 * R : 4 * R].bitcast(FP4X4), w_sc[:, R : 2 * R]),
             )[i]
             nc.tensor.matmul_mx(
                 bank[jt][:],
@@ -167,8 +168,8 @@ def tile_list_msg_relu_bias_kernel(
             codes, plane = hq
             nc.tensor.matmul_mx(
                 acc,
-                lhsT=wd[:, m * P : (m + 1) * P].bitcast(FP8X4),
-                lhsT_scale=wd_sc[:, m * P : (m + 1) * P],
+                lhsT=wd[m].bitcast(FP8X4),
+                lhsT_scale=w_sc[:, 4 * R + m * P : 4 * R + (m + 1) * P],
                 rhs=codes[:].bitcast(FP8X4),
                 rhs_scale=plane[:],
                 start=True,
@@ -183,6 +184,17 @@ def tile_list_msg_relu_bias_kernel(
 
         def store(m, page):
             nc.sync.dma_start(out[m * P : (m + 1) * P, :], page[:])
+
+        for warm in range(4):
+            nc.tensor.matmul_mx(
+                bank[7][:],
+                lhsT=wd[0].bitcast(FP8X4),
+                lhsT_scale=w_sc[:, 4 * R : 4 * R + P],
+                rhs=ws[:, 0 : 2 * R].bitcast(FP4X4),
+                rhs_scale=w_sc[:, 0:R],
+                start=True,
+                stop=True,
+            )
 
         quarter = HALF // 2
         s0, d0, d1, s1 = [], [], [], []
@@ -204,11 +216,14 @@ def tile_list_msg_relu_bias_kernel(
             keep.tile([P, 4 * quarter], BF16, name="h_0", tag="h_0", align_bytes=64),
             keep.tile([P, 4 * quarter], BF16, name="h_1", tag="h_1", align_bytes=64),
         ]
-        for g in range(2):
-            for i, picked in ((1, d0), (2, d1), (3, s1)):
-                for jt in range(2):
-                    mx_pass(2 * g + jt, i, cols(picked[g], jt))
-            hidden(h[g], (2 * g, 2 * g + 1))
+        for i in (1, 2, 3):
+            for jt in range(2):
+                mx_pass(jt, i, cols((s0, d0, d1, s1)[i][0], jt))
+        hidden(h[0], (0, 1))
+        for jt in range(2):
+            for i in (1, 2, 3):
+                mx_pass(2 + jt, i, cols((s0, d0, d1, s1)[i][1], jt))
+        hidden(h[1], (2, 3))
 
 
         d1 = word_tile("d1_y", "d1_y", HALF)

@@ -37,7 +37,7 @@ def tile_list_msg_relu_bias_kernel(
         tab_sc = keep.tile([P, T], U8, name="tab_sc", tag="tab_sc", align_bytes=64)
         ws = keep.tile([P, 2 * 2 * R], U8, name="ws", align_bytes=64)
         w_sc = keep.tile([P, 5 * R], U8, name="w_sc", align_bytes=64)
-        rows = keep.tile([P, 2 * J], U8, name="rows", align_bytes=64)
+        rows = keep.tile([P, 2 * J], U8, name="rows", tag="rows", align_bytes=64)
         planes = [keep.tile([P, 4 * HALF], U8, name="planes%d" % g, align_bytes=64) for g in range(2)]
         wt = keep.tile([P, 2 * R], U32, name="wt", align_bytes=64)
         wd_first = keep.tile([P, P], U32, name="wd_first", align_bytes=64)
@@ -99,12 +99,12 @@ def tile_list_msg_relu_bias_kernel(
             wt_words.rearrange("a p t i -> p a (t i)").bitcast(I32),
         )
         nc.sync.dma_start(ws[:, 2 * R : 4 * R].bitcast(I32), ws_words[1].bitcast(I32))
-        target_planes(1)
-        page_b = keep.tile([P, T], F32, name="page_b", tag="tab_sc", align_bytes=64)
-        nc.gpsimd.memset(page_b[:], 0.0)
         nc.sync.dma_start(wd_rest[:].bitcast(I32), words(wd_words[0])[:, P:N])
         with nc.allow_non_contiguous_dma(reason="one bias value a partition"):
             nc.sync.dma_start(bias[:], b.rearrange("(m p) -> p m", p=P))
+        target_planes(1)
+        page_b = keep.tile([P, T], F32, name="page_b", tag="tab_sc", align_bytes=64)
+        nc.gpsimd.memset(page_b[:], 0.0)
         nc.sync.dma_start(weight[:], wgo)
 
         def gather_words(picked, tab, lst, lo, hi):
@@ -197,64 +197,59 @@ def tile_list_msg_relu_bias_kernel(
             )
 
         quarter = HALF // 2
-        s0, d0, d1, s1 = [], [], [], []
-        for g in range(2):
-            s0.append(word_tile("s0_%d" % g, "s0_%d" % g, quarter))
-            gather_words(s0[g][:], tab0, src_list, g * quarter, (g + 1) * quarter)
-        d0_half = word_tile("d0", "d0", HALF)
-        gather_words(d0_half[:], tab0, dst_list, 0, HALF)
-        d0 = [d0_half[:, g * quarter : (g + 1) * quarter] for g in range(2)]
-        for g in range(2):
-            d1.append(word_tile("d1_%d" % g, "d1_%d" % g, quarter))
-            gather_words(d1[g][:], tab1, dst_list, g * quarter, (g + 1) * quarter)
-            s1.append(word_tile("s1_%d" % g, "s1_%d" % g, quarter))
-            gather_words(s1[g][:], tab1, src_list, g * quarter, (g + 1) * quarter)
-        for g in range(2):
-            for jt in range(2):
-                mx_pass(2 * g + jt, 0, cols(s0[g], jt))
+
+        def pick(picked, tab, lst, lo, hi):
+            gather_words(picked, tab, lst, lo, hi)
+            return [cols(picked, jt) for jt in range((hi - lo) // P)]
+
+        s0 = pick(word_tile("s0", "s0", HALF)[:], tab0, src_list, 0, HALF)
+        d0 = pick(word_tile("d0", "d0", HALF)[:], tab0, dst_list, 0, HALF)
+        d1 = pick(word_tile("d1_a", "d1_a", quarter)[:], tab1, dst_list, 0, quarter)
+        s1 = pick(word_tile("s1_a", "s1_a", quarter)[:], tab1, src_list, 0, quarter)
+        d1 = d1 + pick(word_tile("d1_b", "d1_b", quarter)[:], tab1, dst_list, quarter, HALF)
+        s1 = s1 + pick(word_tile("s1_b", "s1_b", quarter)[:], tab1, src_list, quarter, HALF)
+        d1 = d1 + pick(word_tile("d1_c", "d1_c", HALF)[:], tab1, dst_list, HALF, J)
+        s1 = s1 + pick(word_tile("s1_c", "s1_c", HALF)[:], tab1, src_list, HALF, J)
+        for jt in range(TILES):
+            mx_pass(jt, 0, s0[jt])
         h = [
             keep.tile([P, 4 * quarter], BF16, name="h_0", tag="h_0", align_bytes=64),
             keep.tile([P, 4 * quarter], BF16, name="h_1", tag="h_1", align_bytes=64),
         ]
         for i in (1, 2, 3):
             for jt in range(2):
-                mx_pass(jt, i, cols((s0, d0, d1, s1)[i][0], jt))
+                mx_pass(jt, i, (s0, d0, d1, s1)[i][jt])
         hidden(h[0], (0, 1))
-        for jt in range(2):
+        for jt in (2, 3):
             for i in (1, 2, 3):
-                mx_pass(2 + jt, i, cols((s0, d0, d1, s1)[i][1], jt))
+                mx_pass(jt, i, (s0, d0, d1, s1)[i][jt])
         hidden(h[1], (2, 3))
 
-
-        d1 = word_tile("d1_y", "d1_y", HALF)
-        gather_words(d1[:], tab1, dst_list, HALF, J)
-        s1 = word_tile("s1_y", "s1_y", HALF)
-        gather_words(s1[:], tab1, src_list, HALF, J)
-        s0 = word_tile("s0_y", "d1_0", HALF)
-        gather_words(s0[:], tab0, src_list, HALF, J)
+        s0 = s0 + pick(word_tile("s0_c", "d1_a", quarter)[:], tab0, src_list, HALF, J - quarter)
         hq_a = quantise(h[0], "hq_a", "hq_a")
-        d0 = word_tile("d0_y", "h_0", HALF)
-        gather_words(d0[:], tab0, dst_list, HALF, J)
+        last = word_tile("last", "rows", HALF + quarter)
+        s0 = s0 + pick(last[:, 0:quarter], tab0, src_list, J - quarter, J)
+        d0 = d0 + pick(last[:, quarter:], tab0, dst_list, HALF, J)
         hq_b = quantise(h[1], "hq_b", "hq_b")
         page_c = keep.tile([P, T], F32, name="page_c", tag="h_1", align_bytes=64)
         nc.gpsimd.memset(page_c[:], 0.0)
         pages = (page_a, page_b, page_c)
         y = [keep.tile([P, J], F32, name="y%d" % m) for m in range(1, 4)]
-        y.insert(0, keep.tile([P, J], F32, name="y0", tag="relu3", align_bytes=64))
+        y.insert(0, keep.tile([P, J], F32, name="y0"))
 
         def last_part(tiles, passes):
             for jt in tiles:
                 for i in passes:
-                    mx_pass(TILES + jt, i, cols((s0, d0, d1, s1)[i], jt), 2, 1)
+                    mx_pass(TILES + jt, i, (s0, d0, d1, s1)[i][TILES + jt], 2, 1)
 
         def message(m, hq, lo, hi, acc):
             product(m, hq, acc)
             add_bias(m, y[m][:, lo:hi], acc)
 
-        last_part((0, 1), (2, 3))
         for m in range(2):
             message(m, hq_a, 0, quarter, bank[m][:, 0:quarter])
             place(pages[m], y[m], 0, quarter)
+        last_part((0, 1), (2, 3))
         last_part((0, 1), (0,))
         last_part((2,), (2, 3, 0))
         last_part((0, 1, 2), (1,))

@@ -249,23 +249,26 @@ def tile_list_msg_relu_bias_kernel(
         for m in range(2):
             message(m, hq_a, 0, quarter, bank[m][:, 0:quarter])
             place(pages[m], y[m], 0, quarter)
-        last_part((0, 1), (2, 3))
-        last_part((0, 1), (0,))
+        message(2, hq_a, 0, quarter, bank[2][:, 0:quarter])
+        last_part((0, 1), (2, 3, 0))
+        last_part((0, 1), (1,))
         last_part((2,), (2, 3, 0))
-        last_part((0, 1, 2), (1,))
-        for m in range(2):
-            message(m, hq_b, quarter, HALF, bank[m][:, quarter:HALF])
-            place(pages[m], y[m], quarter, HALF)
-        last_part((3,), (2, 3, 0, 1))
+        last_part((3,), (2,))
+        message(0, hq_b, quarter, HALF, bank[0][:, quarter:HALF])
+        place(pages[0], y[0], quarter, HALF)
+        last_part((2,), (1,))
+        message(1, hq_b, quarter, HALF, bank[1][:, quarter:HALF])
+        place(pages[1], y[1], quarter, HALF)
+        last_part((3,), (3, 0, 1))
         h_c = keep.tile([P, 4 * HALF], BF16, name="h_c", align_bytes=64)
         hidden(h_c, (4, 5, 6, 7))
         hq_c = quantise(h_c, "hq_c", "hq_c")
 
-        for m in (2, 3):
-            product(m, hq_a, bank[m + 2][:, 0:quarter])
-            product(m, hq_b, bank[m + 2][:, quarter:HALF])
-            add_bias(m, y[m][:, 0:HALF], bank[m + 2][:])
+        message(2, hq_b, quarter, HALF, bank[4][:, 0:quarter])
         place(page_c, y[2], 0, HALF)
+        product(3, hq_a, bank[5][:, 0:quarter])
+        product(3, hq_b, bank[5][:, quarter:HALF])
+        add_bias(3, y[3][:, 0:HALF], bank[5][:])
         for m in range(3):
             message(m, hq_c, HALF, J, bank[m][:])
             place(pages[m], y[m], HALF, J)

@@ -99,10 +99,10 @@ def tile_list_msg_relu_bias_kernel(
             wt_words.rearrange("a p t i -> p a (t i)").bitcast(I32),
         )
         nc.sync.dma_start(ws[:, 2 * R : 4 * R].bitcast(I32), ws_words[1].bitcast(I32))
+        target_planes(1)
         nc.sync.dma_start(wd_rest[:].bitcast(I32), words(wd_words[0])[:, P:N])
         with nc.allow_non_contiguous_dma(reason="one bias value a partition"):
             nc.sync.dma_start(bias[:], b.rearrange("(m p) -> p m", p=P))
-        target_planes(1)
         page_b = keep.tile([P, T], F32, name="page_b", tag="tab_sc", align_bytes=64)
         nc.gpsimd.memset(page_b[:], 0.0)
         nc.sync.dma_start(weight[:], wgo)
@@ -138,14 +138,16 @@ def tile_list_msg_relu_bias_kernel(
             return t[:, jt * P : (jt + 1) * P]
 
         def hidden(h, tiles):
-            relu = [keep.tile([P, R], BF16, name="relu%d" % jt, tag="relu%d" % jt, align_bytes=64) for jt in tiles]
+            relu = [keep.tile([P, R], BF16, name="relu%d" % jt, tag="relu%d" % (1 if jt == 2 else jt), align_bytes=64) for jt in tiles]
             turn = [bank[TILES + jt % TILES] for jt in tiles]
             for i, jt in enumerate(tiles):
-                nc.scalar.activation(
-                    relu[i][:].rearrange("j (u p e) -> j u p e", u=2, e=2),
-                    bank[jt][:].rearrange("j (p u e) -> j u p e", u=2, e=2),
-                    ACT.Relu,
-                )
+                pieces = (slice(0, 1), slice(1, 2)) if jt in (1, 7) else (slice(0, 2),)
+                for us in pieces:
+                    nc.scalar.activation(
+                        relu[i][:].rearrange("j (u p e) -> j u p e", u=2, e=2)[:, us],
+                        bank[jt][:].rearrange("j (p u e) -> j u p e", u=2, e=2)[:, us],
+                        ACT.Relu,
+                    )
             for i in range(len(tiles)):
                 pairs = relu[i][:].bitcast(F32)
                 for u in range(2):
@@ -223,19 +225,13 @@ def tile_list_msg_relu_bias_kernel(
         for jt in (2, 3):
             for i in (1, 2, 3):
                 mx_pass(jt, i, (s0, d0, d1, s1)[i][jt])
-        hidden(h[1], (2, 3))
 
         s0 = s0 + pick(word_tile("s0_c", "d1_a", quarter)[:], tab0, src_list, HALF, J - quarter)
         hq_a = quantise(h[0], "hq_a", "hq_a")
-        last = word_tile("last", "rows", HALF + quarter)
+        last = word_tile("last", "d1_b", HALF + quarter)
         s0 = s0 + pick(last[:, 0:quarter], tab0, src_list, J - quarter, J)
         d0 = d0 + pick(last[:, quarter:], tab0, dst_list, HALF, J)
-        hq_b = quantise(h[1], "hq_b", "hq_b")
-        page_c = keep.tile([P, T], F32, name="page_c", tag="h_1", align_bytes=64)
-        nc.gpsimd.memset(page_c[:], 0.0)
-        pages = (page_a, page_b, page_c)
-        y = [keep.tile([P, J], F32, name="y%d" % m) for m in range(1, 4)]
-        y.insert(0, keep.tile([P, J], F32, name="y0"))
+        y = [keep.tile([P, J], F32, name="y%d" % m) for m in (0, 2, 3)]
 
         def last_part(tiles, passes):
             for jt in tiles:
@@ -246,20 +242,27 @@ def tile_list_msg_relu_bias_kernel(
             product(m, hq, acc)
             add_bias(m, y[m][:, lo:hi], acc)
 
-        for m in range(2):
-            message(m, hq_a, 0, quarter, bank[m][:, 0:quarter])
-            place(pages[m], y[m], 0, quarter)
+        last_part((0, 1), (2,))
+        message(0, hq_a, 0, quarter, bank[0][:, 0:quarter])
+        place(page_a, y[0], 0, quarter)
+        hidden(h[1], (2, 3))
+        hq_b = quantise(h[1], "hq_b", "hq_b")
+        page_c = keep.tile([P, T], F32, name="page_c", tag="h_1", align_bytes=64)
+        nc.gpsimd.memset(page_c[:], 0.0)
+        pages = (page_a, page_b, page_c)
+        y.insert(1, keep.tile([P, J], F32, name="y1", tag="relu3", align_bytes=64))
+        message(1, hq_a, 0, quarter, bank[1][:, 0:quarter])
+        place(page_b, y[1], 0, quarter)
         message(2, hq_a, 0, quarter, bank[2][:, 0:quarter])
-        last_part((0, 1), (2, 3, 0))
+        last_part((0, 1), (3, 0))
         last_part((0, 1), (1,))
         last_part((2,), (2, 3, 0))
-        last_part((3,), (2,))
         message(0, hq_b, quarter, HALF, bank[0][:, quarter:HALF])
         place(pages[0], y[0], quarter, HALF)
         last_part((2,), (1,))
         message(1, hq_b, quarter, HALF, bank[1][:, quarter:HALF])
         place(pages[1], y[1], quarter, HALF)
-        last_part((3,), (3, 0, 1))
+        last_part((3,), (2, 3, 0, 1))
         h_c = keep.tile([P, 4 * HALF], BF16, name="h_c", align_bytes=64)
         hidden(h_c, (4, 5, 6, 7))
         hq_c = quantise(h_c, "hq_c", "hq_c")

@@ -46,6 +46,7 @@ def tile_list_msg_relu_bias_kernel(
         weight = keep.tile([P, J], F32, name="weight")
         bias = keep.tile([P, N // P], F32, name="bias")
         page_a = keep.tile([P, T], F32, name="page_a")
+        page_b = keep.tile([P, T], F32, name="page_b")
         bank = [psum.tile([P, R], F32, name="bank%d" % i) for i in range(8)]
 
         ident = keep.tile([P, P], F32, name="ident", align_bytes=64)
@@ -53,8 +54,12 @@ def tile_list_msg_relu_bias_kernel(
         nc.gpsimd.iota(apart[:], [[1, P]], base=0, channel_multiplier=-1, allow_small_or_imprecise_dtypes=True)
         nc.scalar.activation(apart[:], apart[:], ACT.Abs)
         nc.scalar.activation(ident[:], apart[:], ACT.Relu, bias=1.0, scale=-1.0)
-        nc.vector.memset(tab_sc[0:96, :].bitcast(I32), 0)
-        nc.vector.memset(page_a[:].bitcast(I32), 0)
+        nc.vector.memset(tab_sc[0:96, :].bitcast(I32)[:, 0:255], 0)
+        nc.vector.memset(tab_sc[0:96, :].bitcast(I32)[:, 255:512], 0)
+        nc.vector.memset(page_a[:, 0:639].bitcast(I32), 0)
+        nc.vector.memset(page_a[:, 639:1280].bitcast(I32), 0)
+        nc.gpsimd.memset(page_b[:], 0.0)
+        nc.gpsimd.memset(page_a[:, 1280:T].bitcast(I32), 0)
 
         def words(ap):
             return ap.rearrange("p t i -> p (t i)").bitcast(I32)
@@ -103,8 +108,6 @@ def tile_list_msg_relu_bias_kernel(
         nc.sync.dma_start(wd_rest[:].bitcast(I32), words(wd_words[0])[:, P:N])
         with nc.allow_non_contiguous_dma(reason="one bias value a partition"):
             nc.sync.dma_start(bias[:], b.rearrange("(m p) -> p m", p=P))
-        page_b = keep.tile([P, T], F32, name="page_b", tag="tab_sc", align_bytes=64)
-        nc.gpsimd.memset(page_b[:], 0.0)
         nc.sync.dma_start(weight[:], wgo)
 
         def gather_words(picked, tab, lst, lo, hi):
@@ -208,9 +211,8 @@ def tile_list_msg_relu_bias_kernel(
         d0 = pick(word_tile("d0", "d0", HALF)[:], tab0, dst_list, 0, HALF)
         d1 = pick(word_tile("d1_a", "d1_a", quarter)[:], tab1, dst_list, 0, quarter)
         s1 = pick(word_tile("s1_a", "s1_a", quarter)[:], tab1, src_list, 0, quarter)
-        d1 = d1 + pick(word_tile("d1_b", "d1_b", quarter)[:], tab1, dst_list, quarter, HALF)
         s1 = s1 + pick(word_tile("s1_b", "s1_b", quarter)[:], tab1, src_list, quarter, HALF)
-        d1 = d1 + pick(word_tile("d1_c", "d1_c", HALF)[:], tab1, dst_list, HALF, J)
+        d1 = d1 + pick(word_tile("d1_b", "d1_b", J - quarter)[:], tab1, dst_list, quarter, J)
         s1 = s1 + pick(word_tile("s1_c", "s1_c", HALF)[:], tab1, src_list, HALF, J)
         for jt in range(TILES):
             mx_pass(jt, 0, s0[jt])
@@ -222,13 +224,12 @@ def tile_list_msg_relu_bias_kernel(
             for jt in range(2):
                 mx_pass(jt, i, (s0, d0, d1, s1)[i][jt])
         hidden(h[0], (0, 1))
-        for jt in (2, 3):
-            for i in (1, 2, 3):
-                mx_pass(jt, i, (s0, d0, d1, s1)[i][jt])
+        for jt, i in ((2, 1), (3, 1), (2, 3), (2, 2), (3, 3), (3, 2)):
+            mx_pass(jt, i, (s0, d0, d1, s1)[i][jt], 0, 2)
 
         s0 = s0 + pick(word_tile("s0_c", "d1_a", quarter)[:], tab0, src_list, HALF, J - quarter)
         hq_a = quantise(h[0], "hq_a", "hq_a")
-        last = word_tile("last", "d1_b", HALF + quarter)
+        last = word_tile("last", "s1_b", HALF + quarter)
         s0 = s0 + pick(last[:, 0:quarter], tab0, src_list, J - quarter, J)
         d0 = d0 + pick(last[:, quarter:], tab0, dst_list, HALF, J)
         y = [keep.tile([P, J], F32, name="y%d" % m) for m in (0, 2, 3)]

@@ -56,10 +56,10 @@ def tile_list_msg_relu_bias_kernel(
         nc.scalar.activation(ident[:], apart[:], ACT.Relu, bias=1.0, scale=-1.0)
         nc.vector.memset(tab_sc[0:96, :].bitcast(I32)[:, 0:255], 0)
         nc.vector.memset(tab_sc[0:96, :].bitcast(I32)[:, 255:512], 0)
-        nc.vector.memset(page_a[:, 0:639].bitcast(I32), 0)
-        nc.vector.memset(page_a[:, 639:1280].bitcast(I32), 0)
+        nc.vector.memset(page_a[:, 0:383].bitcast(I32), 0)
+        nc.vector.memset(page_a[:, 383:768].bitcast(I32), 0)
         nc.gpsimd.memset(page_b[:], 0.0)
-        nc.gpsimd.memset(page_a[:, 1280:T].bitcast(I32), 0)
+        nc.gpsimd.memset(page_a[:, 768:T].bitcast(I32), 0)
 
         def words(ap):
             return ap.rearrange("p t i -> p (t i)").bitcast(I32)

@@ -60,6 +60,8 @@ def tile_list_msg_relu_bias_kernel(
         nc.vector.memset(page_a[:, 383:768].bitcast(I32), 0)
         nc.gpsimd.memset(page_b[:], 0.0)
         nc.gpsimd.memset(page_a[:, 768:T].bitcast(I32), 0)
+        page_c = keep.tile([P, T], F32, name="page_c", align_bytes=64)
+        nc.gpsimd.memset(page_c[:], 0.0)
 
         def words(ap):
             return ap.rearrange("p t i -> p (t i)").bitcast(I32)
@@ -248,8 +250,6 @@ def tile_list_msg_relu_bias_kernel(
         place(page_a, y[0], 0, quarter)
         hidden(h[1], (2, 3))
         hq_b = quantise(h[1], "hq_b", "hq_b")
-        page_c = keep.tile([P, T], F32, name="page_c", tag="h_1", align_bytes=64)
-        nc.gpsimd.memset(page_c[:], 0.0)
         pages = (page_a, page_b, page_c)
         y.insert(1, keep.tile([P, J], F32, name="y1", tag="relu3", align_bytes=64))
         message(1, hq_a, 0, quarter, bank[1][:, 0:quarter])

@@ -83,8 +83,8 @@ def tile_list_msg_relu_bias_kernel(
                     rows[96 + 8 * q : 96 + 8 * q + 8, :].bitcast(I32).rearrange("p (k g w) -> p g k w", k=2, g=2)[:, g],
                 )
 
-        nc.sync.dma_start(tab_sc[96:P, :].bitcast(I32), by_row(tab_scales))
         nc.sync.dma_start(src_list[:], offs)
+        nc.sync.dma_start(tab_sc[96:P, :].bitcast(I32), by_row(tab_scales))
         nc.sync.dma_start(dst_list[:], offs2)
         lo = 0
         for scales in (ws_scales, wt_scales, wd_scales):

from contextlib import ExitStack

import concourse.mybir as mybir

K, R, N, T, J = 1024, 512, 512, 2048, 1024
FLOPS = 2 * (2 * K * R * J + R * N * J)

F32 = mybir.dt.float32
BF16 = mybir.dt.bfloat16
I32 = mybir.dt.int32
U32 = mybir.dt.uint32
U16 = mybir.dt.uint16
U8 = mybir.dt.uint8
FP8X4 = mybir.dt.float8_e4m3fn_x4
FP4X4 = mybir.dt.float4_e2m1fn_x4
ACT = mybir.ActivationFunctionType
MULT = mybir.AluOpType.mult

P = 128
HALF = J // 2
TILES = HALF // P
LIST_COLS = HALF // 16


def tile_list_msg_relu_bias_kernel(
    tc, tab_words, tab_scales, ws_words, ws_scales, wt_words, wt_scales, wd_words, wd_scales, b, wgo, offs, offs2, out
):
    nc = tc.nc
    with ExitStack() as ctx:
        keep = ctx.enter_context(tc.tile_pool(name="keep", bufs=1))
        psum = ctx.enter_context(tc.psum_pool(name="psum", bufs=1))

        src_list = keep.tile([P, J // 16], U16, name="src_list")
        dst_list = keep.tile([P, J // 16], U16, name="dst_list")
        tab0 = keep.tile([P, T], I32, name="tab0", align_bytes=64)
        tab1 = keep.tile([P, T], I32, name="tab1", align_bytes=64)
        tab_sc = keep.tile([P, T], U8, name="tab_sc", tag="tab_sc", align_bytes=64)
        ws = keep.tile([P, 2 * 2 * R], U8, name="ws", align_bytes=64)
        w_sc = keep.tile([P, 5 * R], U8, name="w_sc", align_bytes=64)
        rows = keep.tile([P, 2 * J], U8, name="rows", tag="rows", align_bytes=64)
        planes = [keep.tile([P, 4 * HALF], U8, name="planes%d" % g, align_bytes=64) for g in range(2)]
        wt = keep.tile([P, 2 * R], U32, name="wt", align_bytes=64)
        wd_first = keep.tile([P, P], U32, name="wd_first", align_bytes=64)
        wd_rest = keep.tile([P, N - P], U32, name="wd_rest", align_bytes=64)
        wd = [wd_first[:]] + [wd_rest[:, m * P : (m + 1) * P] for m in range(N // P - 1)]
        weight = keep.tile([P, J], F32, name="weight")
        bias = keep.tile([P, N // P], F32, name="bias")
        page_a = keep.tile([P, T], F32, name="page_a")
        page_b = keep.tile([P, T], F32, name="page_b")
        bank = [psum.tile([P, R], F32, name="bank%d" % i) for i in range(8)]

        ident = keep.tile([P, P], F32, name="ident", align_bytes=64)
        apart = keep.tile([P, P], F32, name="apart")
        nc.gpsimd.iota(apart[:], [[1, P]], base=0, channel_multiplier=-1, allow_small_or_imprecise_dtypes=True)
        nc.scalar.activation(apart[:], apart[:], ACT.Abs)
        nc.scalar.activation(ident[:], apart[:], ACT.Relu, bias=1.0, scale=-1.0)
        nc.vector.memset(tab_sc[0:96, :].bitcast(I32)[:, 0:255], 0)
        nc.vector.memset(tab_sc[0:96, :].bitcast(I32)[:, 255:512], 0)
        nc.vector.memset(page_a[:, 0:383].bitcast(I32), 0)
        nc.vector.memset(page_a[:, 383:768].bitcast(I32), 0)
        nc.gpsimd.memset(page_b[:], 0.0)
        nc.gpsimd.memset(page_a[:, 768:T].bitcast(I32), 0)
        page_c = keep.tile([P, T], F32, name="page_c", align_bytes=64)
        nc.gpsimd.memset(page_c[:], 0.0)

        def words(ap):
            return ap.rearrange("p t i -> p (t i)").bitcast(I32)

        def by_row(scales):
            return scales.bitcast(I32).rearrange("a s w -> s a w")

        def entries(lst, lo, hi):
            return lst[:, lo // 16 : hi // 16]

        def target_planes(g):
            nc.vector.tensor_copy(
                rows[:, J + g * HALF : J + (g + 1) * HALF],
                tab_sc[:].indirect(entries(dst_list, g * HALF, (g + 1) * HALF)),
            )
            for q in (0, 2, 1, 3):
                nc.sync.dma_start(
                    planes[g][32 * q : 32 * q + 4, :].bitcast(I32).rearrange("p (a k w) -> p a k w", a=2, k=2),
                    rows[96 + 8 * q : 96 + 8 * q + 8, :].bitcast(I32).rearrange("p (k g w) -> p g k w", k=2, g=2)[:, g],
                )

        nc.sync.dma_start(src_list[:], offs)
        nc.sync.dma_start(tab_sc[96:P, :].bitcast(I32), by_row(tab_scales))
        nc.sync.dma_start(dst_list[:], offs2)
        lo = 0
        for scales in (ws_scales, wt_scales, wd_scales):
            passes = scales.shape[0]
            nc.sync.dma_start(
                w_sc[0:16, lo : lo + passes * R].bitcast(I32).rearrange("p (a w) -> p a w", a=passes), by_row(scales)
            )
            lo = lo + passes * R
        nc.sync.dma_start(tab0[:], words(tab_words[0]))
        nc.sync.dma_start(ws[:, 0 : 2 * R].bitcast(I32), ws_words[0].bitcast(I32))
        nc.sync.dma_start(wd_first[:].bitcast(I32), words(wd_words[0])[:, 0:P])
        for q in (2, 1, 3):
            nc.sync.dma_start(w_sc[32 * q : 32 * q + 4, :].bitcast(I32), w_sc[4 * q : 4 * q + 4, :].bitcast(I32))
        nc.sync.dma_start(tab1[:], words(tab_words[1]))
        nc.vector.tensor_copy(rows[:, 0:J], tab_sc[:].indirect(src_list[:]))
        target_planes(0)
        nc.sync.dma_start(
            wt[:].bitcast(I32).rearrange("p (a w) -> p a w", a=2),
            wt_words.rearrange("a p t i -> p a (t i)").bitcast(I32),
        )
        nc.sync.dma_start(ws[:, 2 * R : 4 * R].bitcast(I32), ws_words[1].bitcast(I32))
        target_planes(1)
        nc.sync.dma_start(wd_rest[:].bitcast(I32), words(wd_words[0])[:, P:N])
        with nc.allow_non_contiguous_dma(reason="one bias value a partition"):
            nc.sync.dma_start(bias[:], b.rearrange("(m p) -> p m", p=P))
        nc.sync.dma_start(weight[:], wgo)

        def gather_words(picked, tab, lst, lo, hi):
            nc.vector.tensor_copy(picked, tab[:].bitcast(U32).indirect(entries(lst, lo, hi)))

        def word_tile(name, tag, width):
            return keep.tile([P, width], U32, name=name, tag=tag, align_bytes=64)

        def mx_pass(jt, i, picked, first=0, last=3):
            def picked_plane(a, k):
                lo = (2 * a + k) * HALF + (jt % TILES) * P
                return planes[jt // TILES][:, lo : lo + P]

            plane, w, w_plane = (
                (picked_plane(0, 0), ws[:, 0 : 2 * R].bitcast(FP4X4), w_sc[:, 0:R]),
                (picked_plane(0, 1), wt[:, 0:R].bitcast(FP8X4), w_sc[:, 2 * R : 3 * R]),
                (picked_plane(1, 1), wt[:, R : 2 * R].bitcast(FP8X4), w_sc[:, 3 * R : 4 * R]),
                (picked_plane(1, 0), ws[:, 2 * R : 4 * R].bitcast(FP4X4), w_sc[:, R : 2 * R]),
            )[i]
            nc.tensor.matmul_mx(
                bank[jt][:],
                lhsT=picked.bitcast(FP8X4),
                lhsT_scale=plane,
                rhs=w,
                rhs_scale=w_plane,
                start=(i == first),
                stop=(i == last),
            )

        def cols(t, jt):
            return t[:, jt * P : (jt + 1) * P]

        def hidden(h, tiles):
            relu = [keep.tile([P, R], BF16, name="relu%d" % jt, tag="relu%d" % (1 if jt == 2 else jt), align_bytes=64) for jt in tiles]
            turn = [bank[TILES + jt % TILES] for jt in tiles]
            for i, jt in enumerate(tiles):
                pieces = (slice(0, 1), slice(1, 2)) if jt in (1, 7) else (slice(0, 2),)
                for us in pieces:
                    nc.scalar.activation(
                        relu[i][:].rearrange("j (u p e) -> j u p e", u=2, e=2)[:, us],
                        bank[jt][:].rearrange("j (p u e) -> j u p e", u=2, e=2)[:, us],
                        ACT.Relu,
                    )
            for i in range(len(tiles)):
                pairs = relu[i][:].bitcast(F32)
                for u in range(2):
                    nc.tensor.transpose(turn[i][:, u * P : (u + 1) * P], pairs[:, u * P : (u + 1) * P], ident[:])
            h_pairs = h[:].bitcast(F32)
            for i in range(len(tiles)):
                nc.scalar.copy(
                    h_pairs[:, 2 * P * i : 2 * P * (i + 1)].rearrange("p (j u) -> p j u", u=2),
                    turn[i][:, 0 : 2 * P].rearrange("p (u j) -> p j u", u=2),
                )

        def quantise(h, name, tag):
            width = h.shape[1] // 4
            codes = word_tile(name, tag, width)
            plane = keep.tile([P, width], U8, name=name + "_plane", align_bytes=64)
            nc.vector.quantize_mx(out=codes[:].bitcast(FP8X4), scales=plane[:], in_=h[:])
            return codes, plane

        def product(m, hq, acc):
            codes, plane = hq
            nc.tensor.matmul_mx(
                acc,
                lhsT=wd[m].bitcast(FP8X4),
                lhsT_scale=w_sc[:, 4 * R + m * P : 4 * R + (m + 1) * P],
                rhs=codes[:].bitcast(FP8X4),
                rhs_scale=plane[:],
                start=True,
                stop=True,
            )

        def add_bias(m, y, acc):
            nc.scalar.activation(y, acc, ACT.Identity, bias=bias[:, m : m + 1])

        def place(page, y, lo, hi):
            nc.vector.tensor_tensor(page[:].indirect(entries(dst_list, lo, hi)), y[:, lo:hi], weight[:, lo:hi], MULT)

        def store(m, page):
            nc.sync.dma_start(out[m * P : (m + 1) * P, :], page[:])

        for warm in range(4):
            nc.tensor.matmul_mx(
                bank[7][:],
                lhsT=wd[0].bitcast(FP8X4),
                lhsT_scale=w_sc[:, 4 * R : 4 * R + P],
                rhs=ws[:, 0 : 2 * R].bitcast(FP4X4),
                rhs_scale=w_sc[:, 0:R],
                start=True,
                stop=True,
            )

        quarter = HALF // 2

        def pick(picked, tab, lst, lo, hi):
            gather_words(picked, tab, lst, lo, hi)
            return [cols(picked, jt) for jt in range((hi - lo) // P)]

        s0 = pick(word_tile("s0", "s0", HALF)[:], tab0, src_list, 0, HALF)
        d0 = pick(word_tile("d0", "d0", HALF)[:], tab0, dst_list, 0, HALF)
        d1 = pick(word_tile("d1_a", "d1_a", quarter)[:], tab1, dst_list, 0, quarter)
        s1 = pick(word_tile("s1_a", "s1_a", quarter)[:], tab1, src_list, 0, quarter)
        s1 = s1 + pick(word_tile("s1_b", "s1_b", quarter)[:], tab1, src_list, quarter, HALF)
        d1 = d1 + pick(word_tile("d1_b", "d1_b", J - quarter)[:], tab1, dst_list, quarter, J)
        s1 = s1 + pick(word_tile("s1_c", "s1_c", HALF)[:], tab1, src_list, HALF, J)
        for jt in range(TILES):
            mx_pass(jt, 0, s0[jt])
        h = [
            keep.tile([P, 4 * quarter], BF16, name="h_0", tag="h_0", align_bytes=64),
            keep.tile([P, 4 * quarter], BF16, name="h_1", tag="h_1", align_bytes=64),
        ]
        for i in (1, 2, 3):
            for jt in range(2):
                mx_pass(jt, i, (s0, d0, d1, s1)[i][jt])
        hidden(h[0], (0, 1))
        for jt, i in ((2, 1), (3, 1), (2, 3), (2, 2), (3, 3), (3, 2)):
            mx_pass(jt, i, (s0, d0, d1, s1)[i][jt], 0, 2)

        s0 = s0 + pick(word_tile("s0_c", "d1_a", quarter)[:], tab0, src_list, HALF, J - quarter)
        hq_a = quantise(h[0], "hq_a", "hq_a")
        last = word_tile("last", "s1_b", HALF + quarter)
        s0 = s0 + pick(last[:, 0:quarter], tab0, src_list, J - quarter, J)
        d0 = d0 + pick(last[:, quarter:], tab0, dst_list, HALF, J)
        y = [keep.tile([P, J], F32, name="y%d" % m) for m in (0, 2, 3)]

        def last_part(tiles, passes):
            for jt in tiles:
                for i in passes:
                    mx_pass(TILES + jt, i, (s0, d0, d1, s1)[i][TILES + jt], 2, 1)

        def message(m, hq, lo, hi, acc):
            product(m, hq, acc)
            add_bias(m, y[m][:, lo:hi], acc)

        last_part((0, 1), (2,))
        message(0, hq_a, 0, quarter, bank[0][:, 0:quarter])
        place(page_a, y[0], 0, quarter)
        hidden(h[1], (2, 3))
        hq_b = quantise(h[1], "hq_b", "hq_b")
        pages = (page_a, page_b, page_c)
        y.insert(1, keep.tile([P, J], F32, name="y1", tag="relu3", align_bytes=64))
        message(1, hq_a, 0, quarter, bank[1][:, 0:quarter])
        place(page_b, y[1], 0, quarter)
        message(2, hq_a, 0, quarter, bank[2][:, 0:quarter])
        last_part((0, 1), (3, 0))
        last_part((0, 1), (1,))
        last_part((2,), (2, 3, 0))
        message(0, hq_b, quarter, HALF, bank[0][:, quarter:HALF])
        place(pages[0], y[0], quarter, HALF)
        last_part((2,), (1,))
        message(1, hq_b, quarter, HALF, bank[1][:, quarter:HALF])
        place(pages[1], y[1], quarter, HALF)
        last_part((3,), (2, 3, 0, 1))
        h_c = keep.tile([P, 4 * HALF], BF16, name="h_c", align_bytes=64)
        hidden(h_c, (4, 5, 6, 7))
        hq_c = quantise(h_c, "hq_c", "hq_c")

        message(2, hq_b, quarter, HALF, bank[4][:, 0:quarter])
        place(page_c, y[2], 0, HALF)
        product(3, hq_a, bank[5][:, 0:quarter])
        product(3, hq_b, bank[5][:, quarter:HALF])
        add_bias(3, y[3][:, 0:HALF], bank[5][:])
        for m in range(3):
            message(m, hq_c, HALF, J, bank[m][:])
            place(pages[m], y[m], HALF, J)
            store(m, pages[m])
        message(3, hq_c, HALF, J, bank[3][:])
        place(page_a, y[3], 0, J)
        store(3, page_a)
